import numpy as np, ml_dtypes
CORES = [10,34,74,98]
N = 4
import mx_ref
BF = ml_dtypes.bfloat16
def gentries(a):
    return np.ascontiguousarray(a.reshape(8, 16, -1).transpose(0, 2, 1)).reshape(8, -1)
def gtable(e):
    e = np.asarray(e); return np.ascontiguousarray(e.reshape(8, -1, 16).transpose(0, 2, 1)).reshape(128, -1).astype(np.int32)
def gcols(t, e):
    v = np.concatenate([t.reshape(8, 16, -1, 4), np.zeros((8, 16, 1, 4), BF)], axis=2)
    return np.ascontiguousarray(np.stack([v[g][:, e[g]] for g in range(8)])).reshape(128, -1)
def tile(rs):
    return np.stack(rs, axis=2).reshape(128, -1).astype(BF)
def pick(q, e):
    c = np.concatenate([q[0].reshape(128, -1, 4), np.zeros((128, 1, 4), np.uint8)], axis=1); s = np.concatenate([q[1], np.ones((16, 1), np.uint8)], axis=1)
    return (np.ascontiguousarray(c[:, e].reshape(128, -1)), np.ascontiguousarray(s[:, e]))
def join(*qs):
    return (np.concatenate([q[0] for q in qs], axis=1), np.concatenate([q[1] for q in qs], axis=1))
def put(q, e, v):
    c, s = q[0].reshape(128, -1, 4).copy(), q[1].copy(); c[:, e] = v[0].reshape(128, -1, 4); s[:, e] = v[1]
    return (c.reshape(128, -1), s)
def pk(c, s):
    return (np.ascontiguousarray(c), mx_ref.live(s))
def emit(q):
    return q[0], q[1]
def packed(v, rng):
    q = [mx_ref.quantize(np.ascontiguousarray(v[r])) for r in range(N)]
    return np.stack([a for a, b in q]), np.stack([mx_ref.plane(b, rng) for a, b in q])
def values_of_codes():
    e, c = np.zeros((128, 128, 4), np.float32), np.zeros((128, 2, 4), np.uint8)
    e[np.arange(128), np.arange(128), 0] = 1
    c[:127, :, 0] = np.arange(256).reshape(2, 128).T[:127]
    return mx_ref.matmul(mx_ref.quantize(e.reshape(128, 512).astype(BF)), (c.reshape(128, 8), np.full((16, 2), 127, np.uint8))).T.reshape(-1).astype(np.float64)
CODE_VALUE, SCALE_VALUE = values_of_codes(), 2.0 ** (np.arange(256) - 127.0)
def decode(q):
    return (CODE_VALUE[q[0]].reshape(16, 8, -1, 4) * SCALE_VALUE[q[1]][:, None, :, None] + 0.0).reshape(128, -1).astype(np.float32)
def f(rng, *shape):
    return mx_ref.flush((rng.standard_normal(shape, dtype=np.float32) * np.exp2(rng.integers(-2, 3, shape[:-1] + (1,)))).astype(BF))
def wide(rng, *shape, cols=0):
    v = rng.standard_normal(shape, dtype=np.float32) * np.exp2(rng.integers(-12, 13, shape)).astype(np.float32)
    if cols: v *= np.repeat(np.exp2(rng.integers(-cols, cols + 1, shape[:-2] + (1, shape[-1] // 4))) * (rng.random(shape[:-2] + (1, shape[-1] // 4)) > 0.0625), 4, axis=-1).astype(np.float32)
    return mx_ref.flush(v.astype(BF))
C, M = 384, 8
STEP = [1, 2, 3]
BASE = np.arange(C) // 32 * 32
def big(v):
    v = v.astype(np.float32)
    v[np.abs(v) < np.float32(2.0 ** -16)] = 0
    return v.astype(BF)
def numbers_of(rng):
    return {"x": big(f(rng, N, 128, 4 * C)), "u": np.array(f(rng, N, 128, 512)), "v": np.array(f(rng, N, 128, 512))}
def functions(e):
    return np.stack([gtable(e[r] + BASE) for r in range(N)])
def layers(rng, still=[]):
    w = big(f(rng, N, 128, 2048)).reshape(N, 8, 16, 4, 8, 16, 4)
    for i in still:
        w[:, :, i] = 0
        w[:, :, :, :, :, i] = 0
    return w
def weights(rng, w):
    c, p = packed(np.ascontiguousarray(w).reshape(N, 128, 2048), rng)
    return {"wc": c, "ws": p}
def setup_inputs(rng):
    return {**numbers_of(rng), "fn": functions(rng.integers(0, 32, (N, 8, C))), **weights(rng, layers(rng))}
def setup_inputs_ties(rng):
    d = numbers_of(rng)
    x = d["x"].reshape(N, 8, 16, C, 4)
    even = np.repeat(rng.permutation(C // 32) % 2 == 0, 32)
    k = np.where(even, np.repeat(rng.integers(1, 3, (1, 8, C // 32)), 32, axis=2), rng.integers(0, 3, (N, 8, C)))
    e = rng.integers(0, 32, (N, 8, C))
    e = np.where(even, e[:1], e)
    x[:, :, 0] = 0
    x[:, :, 0, :, 0] = k.astype(np.float32).astype(BF)
    u = d["u"].reshape(N, 128, 128, 4)
    u[:, :, ::16] = 0
    o = rng.permutation(N)
    for r in range(N):
        for h in range(0, 128, 16): u[r, h, h, 0] = 0.0 if r == o[0] else -1.0 if r == o[1] else 1.0
    return {"x": x.reshape(N, 128, 4 * C), "u": u.reshape(N, 128, 512), "v": d["v"], "fn": functions(e), **weights(rng, layers(rng, [0]))}
def setup_inputs_near(rng):
    d = numbers_of(rng)
    x = d["x"].astype(np.float32).reshape(N, 8, 16, C, 4)
    x[:, :, 0] = 0
    x[:, :, 8:] = 0
    far = np.repeat(rng.permutation(C // 32) % 2 == 0, 32)
    c = np.repeat(rng.integers(0, 2, (1, 8, C // 32)) * 2.0 - 1.0, 32, axis=2)
    s = rng.integers(0, 16, (N, 8, C))
    x[:, :, 0, :, 0] = np.where(far, 0.0, c)
    x[:, :, 11, :, 0] = np.where(far, 0.0, 2.0 ** -10)
    x[:, :, 8] = np.where(far[:, None], rng.integers(-1, 2, (N, 8, C, 4)) * 2.0 ** -22, ((s[:, :, :, None] >> np.arange(4)) & 1) * np.exp2(np.arange(4) - 23.0))
    u = d["u"].reshape(N, 128, 128, 4)
    u[:, :, ::16] = 0
    o = rng.permutation(N) % 2
    for r in range(N):
        k = 1.0 if o[r] == 0 else 2.0 ** -30
        for h in range(0, 128, 16):
            u[r, h, h, 0] = k
            u[r, h + 8, h] = k
            u[r, h + 11, h, 0] = k
    return {"x": x.reshape(N, 128, 4 * C).astype(BF), "u": u.reshape(N, 128, 512), "v": d["v"], "fn": functions(rng.integers(0, 32, (N, 8, C))), **weights(rng, layers(rng, [0, 8, 9, 10, 11, 12, 13, 14, 15]))}
def setup_inputs_huge(rng):
    d = numbers_of(rng)
    o = rng.permutation(N)
    k = np.repeat(rng.permutation(C // 32) % 3, 32)
    c = np.where(k == 2, rng.choice([-1.0, 1.0], (N, C)), k * 2.0 - 1.0)
    x = 2.0 ** 30 * (0.6 + 0.4 * rng.random((N, 8, 1, C, 1))) * (1.0 - 0.02 * rng.random((N, 8, 16, C, 4))) * c[:, None, None, :, None]
    a = 2.0 ** 29 * (1.0 - 0.1 * rng.random((N, 8, 16, 8, 4)))
    for g in range(8): a[:, g, :, g] *= 2.0
    for r in range(N):
        if o[r] == 0: a[r] = 2.0 ** 30
        if o[r] % 2 == 1: a[r] *= -1.0
    u = d["u"].reshape(N, 128, 128, 4)
    u[:, :, ::16] = a.reshape(N, 128, 8, 4).astype(np.float32).astype(BF)
    w = np.zeros((N, 128, 4, 128, 4), np.float32)
    i = np.arange(128)
    for b in range(4): w[:, i, b, i, b] = -1
    return {"x": x.astype(np.float32).reshape(N, 128, 4 * C).astype(BF), "u": u.reshape(N, 128, 512), "v": d["v"], "fn": functions(rng.integers(0, 32, (N, 8, C))), **weights(rng, w.astype(BF))}
def setup_inputs_paths(rng):
    d = numbers_of(rng)
    x = d["x"].astype(np.float32).reshape(N, 8, 16, C, 4)
    e, top = np.zeros((N, 8, C // 32, 32), np.int64), np.zeros((N, 8, C // 32), np.int64)
    size = [1, M - 1, M, M + 1, 24, 32]
    o = rng.permutation(8)
    for r in range(N):
        for g in range(8):
            for b in range(C // 32):
                k, a = int(o[r] + g + b) % 8, rng.permutation(32)
                top[r, g, b] = a[0]
                e[r, g, b] = a
                if k == 7: top[r, g, b] = rng.integers(32)
                if k < 6:
                    n = size[k]
                    e[r, g, b] = a[rng.integers(0, n, 32)]
                    e[r, g, b, a[:n]] = np.append(a[1:n], a[n - 1])
    s = rng.integers(0, 3, (N, 8, C // 32, 32)) * 0.5
    np.put_along_axis(s, top[:, :, :, None], 1.5, axis=3)
    x[:, :, 0] = 0
    x[:, :, 0, :, 0] = s.reshape(N, 8, C)
    z = np.exp2(rng.integers(-13, -6, (N, 8, 8, 1, 4)) * 1.0) * (1.0 + (2 * rng.integers(0, 64, (N, 8, 8, 1, 4)) + 1) * 2.0 ** -7) * rng.choice([-1.0, 1.0], (N, 8, 8, 1, 4))
    z[:, :, 0, :, 0] = 1.96875
    x[:, :, 8:] = z
    u = d["u"].reshape(N, 128, 128, 4)
    u[:, :, ::16] = 0
    for h in range(0, 128, 16): u[:, h, h, 0] = 1
    return {"x": x.reshape(N, 128, 4 * C).astype(BF), "u": u.reshape(N, 128, 512), "v": d["v"], "fn": functions(e.reshape(N, 8, C)), **weights(rng, layers(rng, [0, 8, 9, 10, 11, 12, 13, 14, 15]))}
def setup_inputs_spread(rng):
    d = setup_inputs(rng)
    d["x"] = big(wide(rng, N, 128, 4 * C, cols=6))
    return d
def check_inputs(d):
    b = []
    for k in ("x", "u", "v"):
        a = np.abs(d[k].astype(np.float32))
        if not (np.isfinite(a).all() and ((a == 0) | (a >= 2.0 ** -30) & (a <= 2.0 ** 30)).all()): b.append("a value of " + k)
    none, least, most = [emit(mx_ref.quantize(np.full((128, 16), k, np.float32).astype(BF)))[1][0, 0] for k in (0.0, 2.0 ** -30, 2.0 ** 30)]
    for r in range(N):
        if (gentries(d["fn"][r]) // 32 * 32 != BASE).any(): b.append("fn: an entry out of its block")
        if ((d["wc"][r] == 0x7F) | (d["wc"][r] == 0xFF)).any(): b.append("wc: a code that is no number")
        s = mx_ref.live(d["ws"][r])
        if ((s != none) & ((s < least) | (s > most))).any(): b.append("ws: a scale out of range")
    return b
def reread(fun, head):
    row = np.arange(len(fun))
    a = fun
    for k in range(5): a = np.take_along_axis(a, a, axis=1)
    cyc = np.zeros(fun.shape, bool)
    np.put_along_axis(cyc, a, True, axis=1)
    many = np.count_nonzero(cyc, axis=1)
    w = np.take_along_axis(fun, np.argsort(~cyc, axis=1, kind="stable"), axis=1)
    up = fun.copy()
    for j in range(31):
        i = row[j + 1 < many]
        up[i, w[i, j]] = w[i, j + 1]
    root = w[row, many - 1]
    path, at, on = np.full(fun.shape, -1), head, np.ones(len(fun), bool)
    for j in range(32):
        path[:, j] = np.where(on, at, -1)
        on = on & (at != root)
        at = up[row, at]
    q = np.sort(np.where(path < 0, 32, path), axis=1)
    for j in range(32):
        i = row[path[:, j] >= 0]
        up[i, q[i, j]] = path[i, j]
    return up, path
def reference(x, u, v, fn, wc, ws):
    qu = [mx_ref.quantize(u[r]) for r in range(N)]
    lay = [pk(wc[r], ws[r]) for r in range(N)]
    now = [x[r] for r in range(N)]
    fun = np.stack([gentries(fn[r]) - BASE for r in range(N)]).astype(np.int64).reshape(-1, 32)
    row = np.arange(len(fun))
    block = row % (C // 32)
    for t in STEP:
        s = np.stack([mx_ref.matmul(qu[r], mx_ref.quantize(now[r]))[::16] + np.float32(0.0) for r in range(N)])
        fun, path = reread(fun, np.argmax(s.reshape(-1, 32), axis=1))
        to = fun.reshape(N, 8, C) + BASE
        give = np.where(path < 0, -1, path + 32 * block[:, None])[:, :M].reshape(N, 8, -1)
        take = np.full(path.shape, -1)
        for j in range(M):
            i = row[path[:, j] >= 0]
            take[i, path[i, j]] = M * block[i] + j
        take = take.reshape(N, 8, C)
        made, sent = [], []
        for r in range(N):
            z = ((now[r].astype(np.float32) + gcols(now[r], to[r]).astype(np.float32)) * np.float32(0.5)).astype(BF)
            q = mx_ref.quantize(z)
            made.append(tile([mx_ref.matmul(pick(lay[r], np.arange(128 * b, 128 * b + 128)), q) * np.float32(0.03125) + z[:, b::4].astype(np.float32) for b in range(4)]))
            sent.append(mx_ref.quantize(gcols(made[r], give[r])))
        for r in range(N):
            came = gcols(decode(sent[r ^ t]).astype(BF), take[r]).astype(np.float32)
            half = ((made[r].astype(np.float32) + came) * np.float32(0.5)).astype(BF)
            now[r] = np.where(np.repeat(np.repeat(take[r] >= 0, 16, axis=0), 4, axis=1), half, made[r])
    y, fo = np.zeros((N, 128, C), np.float32), np.zeros((N, 8, C), np.float32)
    oc, osc = np.zeros((N, 128, 4 * C), np.uint8), np.zeros((N, 16, C), np.uint8)
    for r in range(N):
        q = mx_ref.quantize(now[r])
        y[r] = mx_ref.matmul(mx_ref.quantize(v[r]), q)
        fo[r] = to[r]
        oc[r], osc[r] = emit(q)
    return {"y": y, "fo": fo, "oc": oc, "osc": osc}

@@ -1,0 +1,475 @@
+from concourse.mybir import dt, AluOpType, AxisListType, ActivationFunctionType
+
+A = AluOpType
+F = ActivationFunctionType
+
+STEP = [1, 2, 3]
+NS = 2
+B = 12 // NS
+H = B // 2
+C = 32 * B
+CW = C + 16
+SL = 8 * B
+XW = 4 * C + 4 * SL
+QW = 128 + SL
+LW = 2 * B + 2
+W2W = 32 + 2 * C
+NB = 8 // NS
+ZS = 1
+BIG = 1.0e29
+TSINK = 900.0
+
+ORDER = "000109072x0203041z05062z202330080a2y0m240n0o0c0e0d0g0b1e1f1d1g0r0q1h0s1m0w210l220z0x33a5353q36100ya73p370i1138271q39280fa80h3a0t0j3b2v3c0va92baa1v3dab0p3e2w3f1wac292r3g2a3h0kas2d3iaradae3k3j2c3l3n3m2h3o342eaf3r1725ag3u3t193vah263s3wai3x12aj4q3y40413z42431i4445ak47am464bal2t48an494aao4c4gap4daqawav4e4f4h2saxa6ay4t4i4u4lazb24jatb04vaub34k4m4w4r4nb1b40u1pb54o2f14b64x4s4p1abs4z4yb7b81j2gb91bba5052bbbd51bc1n53be54551kbi1l32bf5616bvbg572ibj1c18bwbh58bnbkbx59bl5abtbubm15by5hbpbobq5k5l1r5mbz13br5ic01s5n5q5w5j5tc12n2p2l5o315b5r5cc2c45dc3c55s5p5u5vc7c65x5yc8a4c9cd5zca2o1ocb60626164632j1tcccecj1uco65cmckcvcpcnclcf2q1xcycscwcqcxcrczd0ct1y2m5e2kcu5fd16c68d3d4d76d695g66d2d56a676b6e6f6g2u6i6j6kcgch6h6l6mci6o6n706p7172736q6r6sd8d9dc6u6tdedadddf6vdbd66w6xdgdi6ydj6zdhdk76dl77dmdn7a7b747879do7cdpdqdr7d7f7l7i7g7mdt7jdu7e7n7h7kdvdwdxdy7oe2e37pdsdze07r7qe5e1e6e87ued75e47s7te9ebe7eeecekefeaenehelegemeoeiepejeqeres7v817z82807w7x7y838485878889868a8bet8d8c8r8e8s8u8teuevew8f8gex8heyf18j8if2f3f48kezf08lf5f68mf9f78nfa8ofb8xfcf8fd91fffe928y8vfg8zfi8w909996fh9c93fj9a9bflfk97fmfn949d9598fofp9eftfq9i9h9f9gfzfug49k9lfwfv9jg1g2g8fxg0gbg9g3g5gcgegag6gdgffyg7gggkgh8p8q9qfrfs9ogj9r9sgi9p9mgn9t9ngm9ugl9v9w9y9za0a2a19xa3gugvgqgogpgrgsgtgwgxgyh0h1h4h3h2gzh5"
+ON_V = "283p3q5i788y8z95ebej"
+
+BUF = {
+    "fni": (24, "int32", 0), "pi": (16, "int32", 0), "col": (32, "float32", 0), "bits": (8, "float32", 0),
+    "iota1": (CW, "bfloat16", 0), "iotaT": (CW, "float32", 0), "tw0": (CW, "float32", 0),
+    "r16": (64, "bfloat16", 0), "amp": (C, "bfloat16", 0), "r4": (64, "bfloat16", 0), "amp4": (C, "bfloat16", 0),
+    "base": (C, "float32", 0), "locp": (C, "float32", 0), "locq": (C, "float32", 0), "wr": (C, "float32", 0),
+    "rst": (2 * C, "bfloat16", 0), "mrst": (C, "bfloat16", 0), "cc": (C, "float32", 0),
+    "kwin": (CW, "bfloat16", 0), "wsg": (CW, "float32", 0), "wtmp": (C, "float32", 0), "wtmq": (C, "float32", 0), "tab": (192, "float32", 0),
+    "il": (8 * 32, "float32", 0), "cl": (64, "uint16", 0),
+    "half": (512, "bfloat16", 0), "et": (2048, "bfloat16", 0), "ut": (512, "bfloat16", 0), "vt": (512, "bfloat16", 0),
+    "qe": (512, "float8_e4m3fn_x4", 0), "se": (512, "uint8", 0), "qw": (512, "float8_e4m3fn_x4", 0), "sw": (512, "uint8", 0),
+    "qu0": (128, "float8_e4m3fn_x4", 0), "su0": (128, "uint8", 0), "qu": (128, "float8_e4m3fn_x4", 0), "su": (128, "uint8", 0),
+    "qv": (128, "float8_e4m3fn_x4", 0), "sv": (128, "uint8", 0),
+    "qx": (C, "float8_e4m3fn_x4", 1), "sx": (C, "uint8", 1), "qz": (C, "float8_e4m3fn_x4", 1), "sz": (C, "uint8", 1),
+    "qp0": (QW, "float8_e4m3fn_x4", 1), "sp0": (QW, "uint8", 1), "qp1": (QW, "float8_e4m3fn_x4", 1), "sp1": (QW, "uint8", 1),
+    "qp2": (QW, "float8_e4m3fn_x4", 1), "sp2": (QW, "uint8", 1),
+    "xt": (XW, "bfloat16", 1), "xh": (4 * C, "bfloat16", 1), "xg": (4 * C, "bfloat16", 1), "zt": (4 * C, "bfloat16", 1), "z32": (4 * C, "bfloat16", 1),
+    "y32": (4 * CW, "bfloat16", 1), "pt": (512, "bfloat16", 1), "ph": (4 * SL, "bfloat16", 1), "hf": (4 * SL, "bfloat16", 1),
+    "al": (10 * LW, "uint16", 1), "ar": (5 * CW, "bfloat16", 1), "sb": (C, "bfloat16", 1), "sc": (C, "float32", 1),
+    "flf": (32, "float32", 1), "a5": (C, "bfloat16", 1), "eq": (2 * C, "bfloat16", 1), "eqs": (2 * C, "bfloat16", 1),
+    "sm": (8 * 32, "float32", 1), "smi": (64, "int32", 1), "ov": (LW, "uint16", 1),
+    "fp": (CW, "float32", 1), "vw": (CW, "bfloat16", 1), "keep": (C, "bfloat16", 1), "val": (C, "bfloat16", 1),
+    "hb": (CW, "bfloat16", 1), "gg": (C, "float32", 1),
+    "tt": (5 * CW, "float32", 1), "tw": (CW, "float32", 1),
+    "mx": (C, "float32", 1), "junk": (C, "bfloat16", 1), "hc": (8, "float32", 1), "hl": (2, "uint16", 1),
+    "pl": (32, "uint16", 1), "o2": (LW, "uint16", 1), "fl": (C // 4, "uint16", 1), "gl": (LW, "uint16", 1), "sl": (16, "uint16", 1),
+    "w2": (W2W, "bfloat16", 1), "wg": (C, "float32", 1), "fr": (C, "bfloat16", 1), "fot": (C, "float32", 1), "yo": (C, "float32", 1),
+}
+SCRATCH = {k: ("sbuf", [128, v[0] * (NS if v[2] else 1)], v[1]) for k, v in BUF.items()}
+SCRATCH["ps"] = ("psum", [128, 4096], "float32")
+LOADS = ["fn", "u", "v", "wc", "ws"] + ["x%d" % s for s in range(NS)]
+SEMAPHORES = ["cV", "cS", "cP", "cG", "sent", "stored"] + ["ld_" + k for k in LOADS] + ["dup%d" % s for s in range(NS)] + \
+    ["arr%d_%d" % (r, s) for r in range(3) for s in range(NS)]
+
+
+def build(g, T, topo, core, rank):
+    ops = []
+
+    def reg(name, s, a=0, b=None, step=1):
+        w, _, per = BUF[name]
+        o = s * w if per else 0
+        b = w if b is None else b
+        return T[name][:, o + a:o + b:step] if step != 1 else T[name][:, o + a:o + b]
+
+    def add(alts, r, w, s=None, lat=0.0, sem=None, inc=1, arr=None):
+        ops.append({"alts": alts, "r": list(r), "w": list(w), "s": s, "lat": lat, "sem": sem, "inc": inc, "arr": arr})
+
+    def cv(n):
+        return max(64.0, float(n))
+
+    def ts(out, in0, s1, op0, r, w, n, s=None, s2=None, op1=None, gather=False):
+        c = 50 + 1.56 * n if gather else cv(n)
+        if op1 is None:
+            add({"V": (c, lambda: g.vector.tensor_scalar(out, in0, s1, None, op0))}, r, w, s)
+        else:
+            add({"V": (c, lambda: g.vector.tensor_scalar(out, in0, s1, s2, op0, op1))}, r, w, s)
+
+    def tt(out, in0, in1, op, r, w, n, s=None, gather=False, psum=False):
+        c = 50 + 1.7 * n if gather else cv(n if psum else 2 * n)
+        add({"V": (c, lambda: g.vector.tensor_tensor(out, in0, in1, op))}, r, w, s)
+
+    def cp(out, in_, r, w, n, s=None):
+        add({"V": (cv(n), lambda: g.vector.tensor_copy(out, in_))}, r, w, s)
+
+    def ms(out, v, w, n, s=None):
+        add({"V": (cv(n), lambda: g.vector.memset(out, v))}, [], w, s)
+
+    def scan(out, d0, d1, init, op0, op1, r, w, n, s=None):
+        add({"V": (cv(n), lambda: g.vector.tensor_tensor_scan(out, d0, d1, init, op0, op1))}, r, w, s)
+
+    def gat(out, win, off, r, w, n, s=None, scale=None):
+        src = win.indirect(off)
+        if scale is None:
+            add({"V": (50 + 1.56 * n, lambda: g.vector.tensor_copy(out, src)),
+                 "S": (65 + 1.56 * n, lambda: g.scalar.activation(out, src, F.Copy))}, r, w, s)
+        else:
+            add({"V": (50 + 1.56 * n, lambda: g.vector.tensor_scalar(out, src, scale, None, A.mult)),
+                 "S": (65 + 1.56 * n, lambda: g.scalar.activation(out, src, F.Identity, scale=scale))}, r, w, s)
+
+    def mul(out, in_, k, r, w, n, s=None, fast=True):
+        add({"V": (cv(n / 2 if fast else n), lambda: g.vector.tensor_scalar(out, in_, k, None, A.mult)),
+             "S": (cv(n) + 30, lambda: g.scalar.activation(out, in_, F.Identity, scale=k))}, r, w, s)
+
+    def addc(out, in_, colv, r, w, n, s=None):
+        add({"V": (cv(n), lambda: g.vector.tensor_scalar(out, in_, colv, None, A.add)),
+             "S": (cv(n) + 30, lambda: g.scalar.activation(out, in_, F.Identity, bias=colv))}, r, w, s)
+
+    def quant(q, sc, in_, r, w, n, s=None):
+        add({"V": (15 + 0.25 * 4 * n, lambda: g.vector.quantize_mx(q, sc, in_))}, r, w, s)
+
+    def mm(out, lq, ls, rq, rs, r, w, n, s=None, arr=None):
+        add({"P": ((n + 16) * 0.9, lambda: g.tensor.matmul_mx(out, lq, ls, rq, rs, True, True))}, r, w, s, arr=arr)
+
+    def iota(out, pat, base, cm, w, n, flt=True):
+        if flt:
+            add({"G": (130 + 2 * n, lambda: g.iota(out, pat, base, cm, allow_small_or_imprecise_dtypes=True))}, [], w)
+        else:
+            add({"G": (130 + 2 * n, lambda: g.iota(out, pat, base, cm))}, [], w)
+
+    def dma(q, out, in_, r, w, sem, lat, s=None):
+        e = g.sync if q == "Y" else g.scalar
+        add({q: (60.0, lambda: e.dma_start(out, in_))}, r, w, s, lat=lat, sem=sem, inc=16)
+
+    def col(k):
+        return T.col[:, k:k + 1]
+
+    def il(m, a=0, b=32, step=1):
+        return T.il[:, 32 * m + a:32 * m + b:step] if step != 1 else T.il[:, 32 * m + a:32 * m + b]
+
+    def bank(s, t):
+        k = s * NB + t % NB
+        return k * 512, "ps%d" % k
+
+    dma("Y", T.fni[:], T.fn[:], [], ["fni"], "ld_fn", 2000)
+    dma("S", T.ut[:], T.u[:], [], ["ut"], "ld_u", 2200)
+    for s in range(NS):
+        dma("Y" if s % 2 == 0 else "S", reg("xt", s, 0, 4 * C), T.x[:, 4 * C * s:4 * C * (s + 1)], [], ["xt%d" % s], "ld_x%d" % s, 2800, s)
+    dma("Y", T.qw[:].bitcast(dt.uint8), T.wc[:], [], ["qw"], "ld_wc", 3000)
+    dma("Y", T.sw[:], T.ws[:], [], ["sw"], "ld_ws", 2500)
+    dma("Y", T.vt[:], T.v[:], [], ["vt"], "ld_v", 2500)
+
+    iota(T.pi[:, 0:1], [[0, 1]], 0, 1, ["pi0"], 1, False)
+    iota(T.r16[:, 0:16], [[1, 16]], 0, 0, ["r16"], 16)
+    iota(T.iota1[:, 0:C], [[1, C]], 1, 0, ["iota1"], C)
+    iota(il(0), [[16, 32]], 0, 0, ["il0"], 32)
+    iota(T.base[:], [[32, B], [0, 32]], 0, 0, ["base"], C)
+    iota(T.locp[:], [[0, H], [32, 2], [1, 32]], 1, 0, ["locp"], C)
+    iota(T.locq[:], [[0, H], [-32768, 2], [1, 32]], 1, 0, ["locq"], C)
+    iota(il(3), [[32, 16], [0, 2]], -1, 0, ["il3"], 32)
+    iota(il(5), [[0, 16], [16, 2]], 0, 0, ["il5"], 32)
+    iota(T.iotaT[:, 0:C], [[1, C]], 0, 0, ["iotaT"], C)
+    iota(T.r4[:, 0:16], [[0, 4], [1, 4]], 0, 0, ["r4"], 16)
+    iota(T.wr[:], [[32, B], [0, 32]], 32 + C, 0, ["wr"], C)
+    iota(il(6, 0, 16), [[0, 8], [1, 2]], 0, 0, ["il6"], 16)
+    iota(il(7, 0, 4 * H), [[1, 4], [0, H]], 0, 0, ["il7"], 16)
+    ms(T.iota1[:, C:CW], float(C + 1), ["iotap"], 16)
+    ts(T.pi[:, 1:2], T.pi[:, 0:1], 15, A.bitwise_and, ["pi0"], ["pi1"], 1)
+    pj = T.pi[:, 1:2]
+    cp(col(0), pj, ["pi1"], ["c0"], 1)
+    ts(col(1), pj, 1.0, A.add, ["pi1"], ["c1"], 1)
+    ts(col(2), pj, 16.0, A.add, ["pi1"], ["c2"], 1)
+    ts(col(3), pj, 17.0, A.add, ["pi1"], ["c3"], 1)
+    ts(col(20), pj, 15.0, A.is_equal, ["pi1"], ["c20"], 1, s2=255.0, op1=A.mult)
+    ts(col(4), col(20), 1.0, A.add, ["c20"], ["c4"], 1, s2=1.0 / 256, op1=A.mult)
+    ts(col(5), pj, float(B - 1), A.min, ["pi1"], ["c5"], 1, s2=32.0, op1=A.mult)
+    ts(col(6), col(5), -1.0, A.mult, ["c5"], ["c6"], 1, s2=float(C - 32), op1=A.add)
+    ts(col(7), pj, 1.0, A.add, ["pi1"], ["c7"], 1, s2=-1024.0, op1=A.mult)
+    ts(col(8), pj, 17.0, A.add, ["pi1"], ["c8"], 1, s2=-1024.0, op1=A.mult)
+    for m in range(4):
+        ts(T.pi[:, 4 + m:5 + m], T.pi[:, 0:1], m, A.logical_shift_right, ["pi0"], ["pb%d" % m], 1, s2=1, op1=A.bitwise_and)
+    pb = ["pb%d" % m for m in range(4)]
+    ts(T.col[:, 12:16], T.pi[:, 4:8], 5120.0, A.mult, pb, ["c12"], 4, s2=-4096.0, op1=A.add)
+    ts(T.bits[:, 4:8], T.pi[:, 4:8], 1024.0, A.mult, pb, ["bitk"], 4)
+    add({"V": (64.0, lambda: g.vector.tensor_reduce(col(9), T.bits[:, 4:7], AxisListType.X, A.add))}, ["bitk"], ["c9"])
+    add({"V": (64.0, lambda: g.vector.tensor_reduce(col(10), T.bits[:, 4:8], AxisListType.X, A.add))}, ["bitk"], ["c10"])
+    cp(col(11), T.pi[:, 7:8], pb, ["c11"], 1)
+    ts(T.pi[:, 2:3], T.pi[:, 0:1], 3, A.bitwise_and, ["pi0"], ["pi2"], 1)
+    ts(T.pi[:, 3:4], T.pi[:, 0:1], 2, A.logical_shift_right, ["pi0"], ["pi3"], 1, s2=3, op1=A.bitwise_and)
+    ts(col(17), T.pi[:, 2:3], -4.0, A.add, ["pi2"], ["c17"], 1)
+    cp(col(18), T.pi[:, 3:4], ["pi3"], ["c18"], 1)
+    ts(col(19), T.pi[:, 3:4], 1.0, A.add, ["pi3"], ["c19"], 1)
+    ts(col(21), T.pi[:, 3:4], 3.0, A.is_equal, ["pi3"], ["c21"], 1, s2=255.0, op1=A.mult)
+    ts(col(16), col(21), 1.0, A.add, ["c21"], ["c16"], 1, s2=4.0 / 256, op1=A.mult)
+    ts(T.cl[:, 44:44 + 2 * B], il(0, 0, 2 * B), 0.0, A.mult, ["il0", "c0"], ["cl3"], 2 * B, s2=col(0), op1=A.add)
+    for nm, src, c0 in (("amp", "r16", 0), ("amp4", "r4", 18)):
+        w = T[src]
+        ts(w[:, 16:32], w[:, 0:16], col(c0), A.not_equal, [src, "c%d" % c0], [src + "a"], 16)
+        ts(w[:, 32:48], w[:, 0:16], col(c0 + 1), A.is_equal, [src, "c%d" % (c0 + 1)], [src + "b"], 16, s2=255.0, op1=A.mult)
+        tt(w[:, 48:64], w[:, 16:32], w[:, 32:48], A.add, [src + "a", src + "b"], [src + "c"], 16)
+        gat(T[nm][:], w[:, 48:64], T.cl[:, 44:44 + 2 * B], [src + "c", "cl3"], [nm], C)
+    ts(il(1), il(0), col(1), A.add, ["il0", "c1"], ["il1"], 32)
+    ts(il(2), il(0), col(0), A.add, ["il0", "c0"], ["il2"], 32, s2=32.0, op1=A.add)
+    ts(il(4), il(0), col(0), A.add, ["il0", "c0"], ["il4"], 32, s2=float(C), op1=A.add)
+    ts(T.cl[:, 0:32], il(5), col(0), A.add, ["il5", "c0"], ["cl0"], 32)
+    cp(T.cl[:, 32:40], il(0, 0, 8), ["il0"], ["cl1"], 8)
+    ts(il(6, 16, 32), il(6, 0, 16), col(11), A.not_equal, ["il6", "c11"], ["il6b"], 16, s2=-4096.0, op1=A.mult)
+    ts(il(6, 0, 16), il(6, 16, 32), col(9), A.subtract, ["il6b", "c9"], ["il6"], 16)
+    ms(il(7, 16, 32), 0.0, ["il7b"], 16)
+    ts(il(7, 16, 16 + 4 * H), il(7, 0, 4 * H), 0.25, A.mult, ["il7"], ["il7b"], 16)
+    ts(T.tab[:, 0:16], T.r16[:, 0:16], col(0), A.is_le, ["r16", "c0"], ["tab0"], 16)
+    add({"V": (64.0, lambda: g.vector.tensor_reduce(col(22), T.tab[:, H:16:H], AxisListType.X, A.add))}, ["tab0"], ["c22"])
+    ts(col(23), col(22), float(-H), A.mult, ["c22", "c0"], ["c23"], 1, s2=col(0), op1=A.add)
+    cp(T.cl[:, 40:41], col(23), ["c23"], ["cl2"], 1)
+    ms(T.rst[:], 1.0, ["rst"], C)
+    ms(T.rst[:, 0:2 * C:32], 0.0, ["rst"], 2 * B)
+    ms(T.mrst[:], 0.0, ["mrst"], C / 2)
+    ms(T.mrst[:, 0:C:32], 2.0 ** 20, ["mrst"], B)
+    ms(T.kwin[:], 0.0, ["kwin"], CW / 2)
+    ms(T.kwin[:, 0:1], 1.0, ["kwin"], 1)
+    ts(T.wtmq[:], T.base[:], col(5), A.is_equal, ["base", "c5"], ["wtmq"], C, s2=-0.5, op1=A.add)
+    mul(T.cc[:], T.wtmq[:], 2 * BIG, ["wtmq"], ["cc"], C, fast=False)
+    ms(T.iotaT[:, C:CW], TSINK, ["iotaTp"], 16)
+    addc(T.tw0[:], T.iotaT[:], col(12), ["iotaT", "iotaTp", "c12"], ["tw0"], CW)
+    lo = T.locp[:, 0:32]
+    ts(T.tab[:, 0:32], lo, col(0), A.is_le, ["locp", "c0"], ["tab0"], 32)
+    ts(T.tab[:, 32:64], lo, col(2), A.is_le, ["locp", "c2"], ["tab1"], 32, s2=1024.0, op1=A.mult)
+    ts(T.tab[:, 64:96], lo, col(1), A.is_equal, ["locp", "c1"], ["tab2"], 32)
+    ts(T.tab[:, 96:128], lo, col(3), A.is_equal, ["locp", "c3"], ["tab3"], 32, s2=1024.0, op1=A.mult)
+    tt(T.tab[:, 128:160], T.tab[:, 0:32], T.tab[:, 32:64], A.add, ["tab0", "tab1"], ["tab4"], 32)
+    tt(T.tab[:, 160:192], T.tab[:, 64:96], T.tab[:, 96:128], A.add, ["tab2", "tab3"], ["tab5"], 32)
+    tt(T.wtmp[:], T.tab[:, 160:192].indirect(T.cl[:, 0:2 * B]), T.wr[:], A.mult, ["tab5", "cl0", "wr"], ["wtmp"], C, gather=True)
+    tt(T.wsg[:, 0:C], T.tab[:, 128:160].indirect(T.cl[:, 0:2 * B]), T.wtmp[:], A.add, ["tab4", "cl0", "wtmp"], ["wsg"], C, gather=True)
+    ms(T.wsg[:, C:CW], 0.0, ["wsgp"], 16)
+    ms(T.half[:], 0.5, ["half"], 256)
+    for b in range(4):
+        add({"G": (170 + 2 * 512, lambda b=b: g.affine_select(T.et[:, 512 * b:512 * b + 512], T.half[:], [[8, 128], [1, 4]], A.is_equal, 0.0, -b, -8))},
+            ["half"], ["et%d" % b])
+        quant(T.qe[:, 128 * b:128 * b + 128], T.se[:, 128 * b:128 * b + 128], T.et[:, 512 * b:512 * b + 512], ["et%d" % b], ["qe%d" % b], 128)
+    quant(T.qu0[:], T.su0[:], T.ut[:], ["ut"], ["qu0"], 128)
+    add({"V": (250.0, lambda: g.vector.tensor_copy(T.qu[:].bitcast(dt.uint32), T.qu0[:].bitcast(dt.uint32).indirect(T.cl[:, 32:40])))}, ["qu0", "cl1"], ["qu"])
+    add({"S": (265.0, lambda: g.scalar.activation(T.su[:], T.su0[:].indirect(T.cl[:, 32:40]), F.Copy))}, ["qu0", "cl1"], ["su"])
+    quant(T.qv[:], T.sv[:], T.vt[:], ["vt"], ["qv"], 128)
+    for s in range(NS):
+        iota(reg("pt", s, 4 * SL, 512), [[0, 512 - 4 * SL]], 0, 0, ["ptz%d" % s], 512 - 4 * SL)
+    ms(T.al[:], C, ["alz"], 5 * LW * NS)
+    ms(T.hb[:, 0:NS * CW:CW], 0.0, ["hb0"], 1)
+    ms(T.vw[:, 0:NS * CW:CW], 0.0, ["vw0"], 1)
+    ms(T.fp[:, 0:NS * CW:CW], 2.0 ** 17, ["fp0"], 1)
+    ms(T.y32[:, C:4 * CW * NS:CW], 0.0, ["yz"], 8)
+
+    def stream(s):
+        def k(name):
+            return "%s%s" % (name, "_%d" % s)
+
+        def al(m, n=2 * B):
+            return reg("al", s, m * LW, m * LW + n)
+
+        def ar(m, n=CW):
+            return reg("ar", s, m * CW, m * CW + n)
+
+        def tb(m, n=CW):
+            return reg("tt", s, m * CW, m * CW + n)
+
+        def sm(m, a=0, b=2 * B, step=1):
+            return reg("sm", s, 32 * m + a, 32 * m + b, step)
+
+        def tolist(out, row, r, w):
+            scan(reg("sb", s), T.amp[:], row, 0.0, A.mult, A.max, r + ["amp"], [k("sb")], C / 2, s)
+            ts(out, reg("sb", s, 15, C, 16), col(4), A.mult, [k("sb"), "c4", "alz"], w, 2 * B, s, s2=-1.0, op1=A.add)
+
+        X = "xt%d" % s
+        ms(reg("w2", s, 0, 32), 1.0, [k("w2p")], 32, s)
+
+        fs = T.fni[:, 2 * B * s:2 * B * (s + 1)]
+        ts(al(0), fs, float(s * C), A.subtract, ["fni", "alz"], [k("al0")], 2 * B, s)
+        ts(reg("flf", s, 0, 2 * B), fs, float(s * C), A.subtract, ["fni"], [k("flf")], 2 * B, s)
+        gat(ar(0, C), T.iota1[:, 0:C], al(0), ["iota1", k("al0")], [k("ar0")], C, s)
+        for m in range(4):
+            gat(ar(m + 1, C), ar(m, C), al(m), [k("ar%d" % m), k("al%d" % m)], [k("ar%d" % (m + 1))], C, s)
+            tolist(al(m + 1), ar(m + 1, C), [k("ar%d" % (m + 1))], [k("al%d" % (m + 1))])
+        tt(reg("a5", s), ar(4, C).indirect(al(4)), T.base[:], A.subtract, [k("ar4"), k("al4"), "base"], [k("a5")], C, s, gather=True)
+        for e in range(2):
+            ts(reg("eq", s, e * C, e * C + C), reg("a5", s), col(1 + 2 * e), A.is_equal, [k("a5"), "c%d" % (1 + 2 * e)], [k("eq%d" % e)], C / 2, s)
+        scan(reg("eqs", s), T.rst[:], reg("eq", s), 0.0, A.mult, A.max, ["rst", k("eq0"), k("eq1")], [k("eqs0"), k("eqs1")], C, s)
+        for e in range(2):
+            tt(sm(0, e, 2 * B, 2), reg("eqs", s, e * C + 31, e * C + C, 32), il(1, e, 2 * B, 2), A.mult, [k("eqs%d" % e), "il1"], [k("sm0%d" % e)], B, s)
+        cp(reg("ov", s, 0, 2 * B), sm(0), [k("sm00"), k("sm01")], [k("ov")], 2 * B, s)
+        ov = reg("ov", s, 0, 2 * B)
+        gat(reg("fp", s, 1, C + 1), T.locq[:], al(0), ["locq", k("al0")], [k("fp")], C, s)
+        gat(reg("vw", s, 1, C + 1), T.locp[:], al(0), ["locp", k("al0")], [k("vw")], C, s, scale=1024.0)
+        ts(sm(1), sm(0), 0.0, A.is_gt, [k("sm00"), k("sm01")], [k("sm1")], 2 * B, s, s2=float(C), op1=A.mult)
+        tt(sm(2), sm(1), reg("flf", s, 0, 2 * B), A.max, [k("sm1"), k("flf")], [k("sm2")], 2 * B, s)
+        gat(reg("keep", s), T.kwin[:], ov, ["kwin", k("ov")], [k("keep")], C, s)
+        gat(reg("val", s), reg("vw", s, 0, C + 1), ov, [k("vw"), "vw0", k("ov")], [k("val")], C, s)
+        scan(reg("hb", s, 1, C + 1), reg("keep", s), reg("val", s), 0.0, A.mult, A.add, [k("keep"), k("val")], [k("hb")], C / 2, s)
+        tt(reg("gg", s), reg("fp", s, 0, C + 1).indirect(ov), reg("hb", s, 0, C), A.add, [k("fp"), "fp0", k("ov"), k("hb"), "hb0"], [k("gg")], C, s, gather=True)
+        for e in range(2):
+            o, cb = reg("eq", s, e * C, e * C + C), col(7 + e)
+            add({"S": (C + 30.0, lambda o=o, cb=cb: g.scalar.activation(o, reg("gg", s), F.Abs, bias=cb))}, [k("gg"), "c%d" % (7 + e)], [k("eq%d" % e)], s)
+            scan(reg("eqs", s, e * C, e * C + C), T.mrst[:], o, 0.0, A.max, A.min, ["mrst", k("eq%d" % e)], [k("eqs%d" % e)], C / 2, s)
+            tt(sm(3, e, 2 * B, 2), reg("eqs", s, e * C + 31, e * C + C, 32), il(3, e, 2 * B, 2), A.add, [k("eqs%d" % e), "il3"], [k("sm3%d" % e)], B, s)
+        tt(sm(4), sm(3), sm(2), A.min, [k("sm30"), k("sm31"), k("sm2")], [k("sm4")], 2 * B, s)
+        cp(al(5), sm(4), [k("sm4"), "alz"], [k("al5")], 2 * B, s)
+        n1 = 2 * B + 1
+        par = reg("w2", s, 32, 32 + CW)
+        gat(par, T.iota1[:], al(5, n1), ["iota1", "iotap", k("al5")], [k("w2a"), k("w2b")], CW, s)
+        for m in range(4):
+            lk = [k("al%d" % (5 + m))]
+            if m == 0:
+                gat(ar(1), par, al(5, n1), [k("w2a"), k("w2b")] + lk, [k("ar1")], CW, s)
+                tt(tb(0), T.tw0[:].indirect(al(5, n1)), T.iotaT[:], A.max, ["tw0", "iotaT", "iotaTp"] + lk, [k("tt0")], CW, s, gather=True)
+            else:
+                gat(ar(m + 1), ar(m), al(5 + m, n1), [k("ar%d" % m)] + lk, [k("ar%d" % (m + 1))], CW, s)
+                addc(reg("tw", s), tb(m - 1), col(12 + m), [k("tt%d" % (m - 1)), "c12"], [k("tw")], CW, s)
+                tt(tb(m), reg("tw", s).indirect(al(5 + m, n1)), tb(m - 1), A.max, [k("tw"), k("tt%d" % (m - 1))] + lk, [k("tt%d" % m)], CW, s, gather=True)
+            tolist(al(6 + m), ar(m + 1, C), [k("ar%d" % (m + 1))], [k("al%d" % (6 + m))])
+        gat(tb(4, C), tb(3), al(9), [k("tt3"), k("al9")], [k("tt4")], C, s)
+
+        qx, sx, qz, sz = reg("qx", s), reg("sx", s), reg("qz", s), reg("sz", s)
+        for rd in range(3):
+            quant(qx, sx, reg("xt", s, 0, 4 * C), [X], [k("qx")], C, s)
+            mul(reg("xh", s), reg("xt", s, 0, 4 * C), 0.5, [X], [k("xh")], 4 * C, s)
+            dma("Y", reg("xg", s), reg("xh", s), [k("xh")], [k("xg")], "dup%d" % s, 2500, s)
+            o, bk = bank(s, 0)
+            mm(T.ps[:, o:o + C], T.qu[:], T.su[:], qx, sx, ["qu", "su", k("qx")], [bk], C, s)
+            scan(reg("mx", s), T.ps[:, o:o + C], T.cc[:], -BIG, A.max, A.min, ["cc"], [bk, k("mx")], C, s)
+            add({"V": (64.0, lambda: g.vector.tensor_reduce(reg("hc", s, 0, 1), reg("mx", s, 31, C, 32), AxisListType.X, A.max))}, [k("mx")], [k("hc0")], s)
+            add({"S": (C + 50.0, lambda: g.scalar.activation(reg("junk", s), reg("mx", s), F.Sign, bias=reg("hc", s, 0, 1), scale=-1.0, accum_out=reg("hc", s, 4, 5)))},
+                [k("mx"), k("hc0")], [k("junk"), k("hc1")], s)
+            ts(reg("hl", s, 0, 1), reg("hc", s, 4, 5), col(6), A.subtract, [k("hc1"), "c6"], [k("hl")], 1, s)
+            hl = reg("hl", s, 0, 1)
+            for e in range(2):
+                ts(reg("pl", s, e, 32, 2), tb(3 + e, C).indirect(hl), col(10), A.subtract, [k("tt%d" % (3 + e)), k("hl"), "c10"], [k("pl%d" % e)], 16, s,
+                   s2=float(C), op1=A.min, gather=True)
+            pl = reg("pl", s, 0, 2 * B)
+            pk = [k("pl0"), k("pl1")]
+            gat(reg("wg", s), T.wsg[:], pl, ["wsg", "wsgp"] + pk, [k("wg")], C, s)
+            gat(reg("w2", s, 32 + C, W2W), T.iota1[:], pl, ["iota1", "iotap"] + pk, [k("w2b")], C, s)
+            scan(reg("sc", s), T.rst[:, 0:C], reg("wg", s), 0.0, A.mult, A.add, ["rst", k("wg")], [k("sc")], C, s)
+            cp(reg("smi", s, 0, B), reg("sc", s, 31, C, 32), [k("sc")], [k("si")], B, s)
+            ts(reg("smi", s, 32, 32 + 2 * B, 2), reg("smi", s, 0, B), 1023, A.bitwise_and, [k("si")], [k("q0")], B, s)
+            ts(reg("smi", s, 33, 32 + 2 * B, 2), reg("smi", s, 0, B), 10, A.logical_shift_right, [k("si")], [k("q1")], B, s)
+            tt(sm(5), reg("smi", s, 32, 32 + 2 * B), il(2, 0, 2 * B), A.max, [k("q0"), k("q1"), "il2"], [k("sm5")], 2 * B, s)
+            cp(reg("o2", s, 0, 2 * B), sm(5), [k("sm5")], [k("o2")], 2 * B, s)
+            gat(reg("fr", s), reg("w2", s), reg("o2", s, 0, 2 * B), [k("w2p"), k("w2a"), k("w2b"), k("o2")], [k("fr")], C, s)
+            scan(reg("sb", s), T.amp4[:], reg("fr", s), 0.0, A.mult, A.max, [k("fr"), "amp4"], [k("sb")], C / 2, s)
+            ts(reg("fl", s), reg("sb", s, 3, C, 4), col(16), A.mult, [k("sb"), "c16", "c17"], [k("fl")], C // 4, s, s2=col(17), op1=A.add)
+            if rd == 2:
+                ts(reg("fot", s), reg("fr", s), float(s * C - 1), A.add, [k("fr")], [k("fot")], C, s)
+                dma("Y", T.fo[:, s * C:s * C + C], T.fot[0:128:16, s * C:s * C + C], [k("fot")], [], "stored", 2000, s)
+            tt(sm(6, 0, 16), tb(2, C).indirect(hl), il(6, 0, 16), A.add, [k("tt2"), k("hl"), "il6"], [k("sm6")], 16, s, gather=True)
+            tt(sm(7, 0, H), sm(6, 0, B, 2), sm(6, 1, B, 2), A.max, [k("sm6")], [k("sm7a")], H, s)
+            ts(reg("gl", s, 0, H), sm(7, 0, H), float(C), A.min, [k("sm7a")], [k("gl")], H, s)
+            tt(sm(7, 8, 8 + H), sm(7, 0, H), il(4, 0, H), A.min, [k("sm7a"), "il4"], [k("sm7b")], H, s)
+            tt(sm(7, 16, 32), sm(7, 8, 8 + H).indirect(T.cl[:, 40:41]), il(7, 16, 32), A.add, [k("sm7b"), "cl2", "il7b"], [k("sm7c")], 16, s, gather=True)
+            ts(reg("sl", s), sm(7, 16, 32), 4.0, A.mult, [k("sm7c")], [k("sl")], 16, s)
+            zk = [k("zt%d" % z) for z in range(ZS)]
+            for z in range(ZS):
+                a, b = 4 * C * z // ZS, 4 * C * (z + 1) // ZS
+                tt(reg("zt", s, a, b), reg("xh", s).indirect(reg("fl", s, a // 16, b // 16)), reg("xg", s, a, b), A.add, [k("xh"), k("xg"), k("fl")], [zk[z]], b - a, s, gather=True)
+            for t in range(4):
+                mul(reg("z32", s, t * C, t * C + C), reg("zt", s, t, 4 * C, 4), 32.0, zk, [k("z32%d" % t)], C, s)
+            quant(qz, sz, reg("zt", s), zk, [k("qz")], C, s)
+            for t in range(4):
+                o, bk = bank(s, t)
+                mm(T.ps[:, o:o + C], T.qw[:, 128 * t:128 * t + 128], T.sw[:, 128 * t:128 * t + 128], qz, sz, ["qw", "sw", k("qz")], [bk], C, s)
+                tt(reg("y32", s, t * CW, t * CW + C), T.ps[:, o:o + C], reg("z32", s, t * C, t * C + C), A.add, [k("z32%d" % t)], [bk, k("y%d" % t)], C, s, psum=True)
+                gat(reg("pt", s, t, 4 * SL, 4), reg("y32", s, t * CW, t * CW + C + 1), reg("gl", s, 0, H), [k("y%d" % t), k("gl"), "yz"], [k("pt%d" % t)], SL, s, scale=0.03125)
+            qp, sp = "qp%d" % rd, "sp%d" % rd
+            pts = [k("pt%d" % t) for t in range(4)]
+            quant(reg(qp, s, 0, 128), reg(sp, s, 0, 128), reg("pt", s), pts + ["ptz%d" % s], [k(qp)], 128, s)
+            peer = T.cores[rank ^ STEP[rd]]
+            rid, pid, _ = topo.addr(peer)
+            mask = topo.mask(core, peer)
+            sem = T.sem["arr%d_%d" % (rd, s)]
+            ne = len(topo.engines(core, peer))
+
+            def send(qp=qp, sp=sp, rid=rid, pid=pid, mask=mask, sem=sem):
+                g.remote_dma(reg(qp, s, 128, QW).bitcast(dt.uint8), reg(qp, s, 0, SL).bitcast(dt.uint8), sem, T.sem.sent, pid, rid, mask)
+                g.remote_dma(reg(sp, s, 128, QW), reg(sp, s, 0, SL), sem, T.sem.sent, pid, rid, mask)
+                return None
+            add({"G": (1200.0, send)}, [k(qp)], [k("fly%d" % rd)], s, lat=2200.0, sem="remote", inc=2 * ne)
+            mul(reg("ph", s), reg("pt", s, 0, 4 * SL), 0.5, pts, [k("ph")], 4 * SL, s)
+            for t in range(4):
+                mul(reg("xt", s, t, 4 * C, 4), reg("y32", s, t * CW, t * CW + C), 0.03125, [k("y%d" % t)], [X, k("xw%d" % t)] if t == 0 else [k("xw%d" % t)], C, s)
+                if t > 0:
+                    ops[-1]["r"].append(k("xw0"))
+            for t in range(4):
+                o, bk = bank(s, t)
+                mm(T.ps[:, o:o + 128], T.qe[:, 128 * t:128 * t + 128], T.se[:, 128 * t:128 * t + 128], reg(qp, s, SL, QW), reg(sp, s, SL, QW),
+                   ["qe%d" % t, k(qp), k("fly%d" % rd)], [bk], 128, s, arr=(sem, 2 * ne))
+                tt(reg("hf", s, t * SL, t * SL + SL), T.ps[:, o + 128 - SL:o + 128], reg("ph", s, t, 4 * SL, 4), A.add, [k("ph")], [bk, k("hf%d" % t)], SL, s, psum=True)
+            add({"V": (50 + 3.8 * 4 * SL, lambda: g.vector.tensor_copy(reg("xt", s).indirect(reg("sl", s, 0, 2 * B)), reg("hf", s)))},
+                [k("hf%d" % t) for t in range(4)] + [k("sl")] + [k("xw%d" % t) for t in range(4)], [X], s)
+        quant(qx, sx, reg("xt", s, 0, 4 * C), [X], [k("qx")], C, s)
+        o, bk = bank(s, 0)
+        mm(T.ps[:, o:o + C], T.qv[:], T.sv[:], qx, sx, ["qv", k("qx")], [bk], C, s)
+        add({"V": (cv(C), lambda: g.vector.tensor_copy(reg("yo", s), T.ps[:, o:o + C])),
+             "S": (cv(C) + 30, lambda: g.scalar.activation(reg("yo", s), T.ps[:, o:o + C], F.Copy))}, [], [bk, k("yo")], s)
+        dma("Y", T.oc[:, 4 * s * C:4 * s * C + 4 * C], qx.bitcast(dt.uint8), [k("qx")], [], "stored", 2200, s)
+        for q in range(4):
+            dma("Y", T.osc[4 * q:4 * q + 4, s * C:s * C + C], T.sx[32 * q:32 * q + 4, s * C:s * C + C], [k("qx")], [], "stored", 2000, s)
+        dma("S", T.y[:, s * C:s * C + C], reg("yo", s), [k("yo")], [], "stored", 2200, s)
+
+    for s in range(NS):
+        stream(s)
+    return ops
+
+
+def deps(ops):
+    last, readers = {}, {}
+    pred = [set() for _ in ops]
+    for i, o in enumerate(ops):
+        for key in o["r"]:
+            if key in last:
+                pred[i].add(last[key])
+        for key in o["w"]:
+            if key in last:
+                pred[i].add(last[key])
+            for j in readers.get(key, []):
+                pred[i].add(j)
+        for key in o["r"]:
+            readers.setdefault(key, []).append(i)
+        for key in o["w"]:
+            last[key] = i
+            readers[key] = []
+        pred[i].discard(i)
+    return pred
+
+
+def digits(text):
+    return [int(text[a:a + 2], 36) for a in range(0, len(text), 2)]
+
+
+def rank_program(g, core, T, topo):
+    rank = T.rank_of(core)
+    if rank is None:
+        return
+    ops = build(g, T, topo, core, rank)
+    pred = deps(ops)
+    order = digits(ORDER) if ORDER else list(range(len(ops)))
+    on_v = set(digits(ON_V))
+    place = {i: a for a, i in enumerate(order)}
+    queue = {"V": g.vector, "S": g.scalar, "P": g.tensor, "G": g, "Y": g.sync}
+    count = {}
+    mark = [None] * len(ops)
+    clock = [None] * len(ops)
+    known = {e: {} for e in queue}
+    for i in order:
+        o = ops[i]
+        e = list(o["alts"])[0] if len(o["alts"]) == 1 else ("V" if i in on_v else "S")
+        q, kn = queue[e], known[e]
+        need = {}
+        for j in pred[i]:
+            if mark[j] is not None:
+                sname, c = mark[j]
+                if kn.get(sname, 0) < c and need.get(sname, (0, 0))[0] < c:
+                    need[sname] = (c, j)
+        for sname, (c, j) in sorted(need.items(), key=lambda kv: -place[kv[1][1]]):
+            if kn.get(sname, 0) < c:
+                q.wait_ge(T.sem[sname], c)
+                for a, b in clock[j].items():
+                    if kn.get(a, 0) < b:
+                        kn[a] = b
+        if o["arr"] is not None:
+            sem, c = o["arr"]
+            tag = "arr:%s:%s" % (o["r"][-1], e)
+            if tag not in kn:
+                q.wait_ge(sem, c)
+                kn[tag] = 1
+        ins = o["alts"][e][1]()
+        if o["sem"] == "remote":
+            count["sent"] = count.get("sent", 0) + o["inc"]
+            continue
+        sname = o["sem"] or "c" + e
+        count[sname] = count.get(sname, 0) + o["inc"]
+        ins.then_inc(T.sem[sname], o["inc"])
+        mark[i] = (sname, count[sname])
+        clock[i] = dict(kn)
+        clock[i][sname] = count[sname]
+    for sname in ["cG", "cP", "cS", "cV", "sent", "stored"]:
+        g.wait_ge(T.sem[sname], count[sname])

@@ -6,51 +6,47 @@ F = ActivationFunctionType
 STEP = [1, 2, 3]
 NS = 2
 B = 12 // NS
-H = B // 2
 C = 32 * B
 CW = C + 16
 SL = 8 * B
 XW = 4 * C + 4 * SL
 QW = 128 + SL
-LW = 2 * B + 2
-W2W = 32 + 2 * C
+LW = 2 * B
+W2W = CW + C
 NB = 8 // NS
-ZS = 1
+RO = 16
+SH = 144
 BIG = 1.0e29
-TSINK = 900.0
+TSINK = 100000.0
 
-ORDER = "000109072x0203041z05062z202330080a2y0m240n0o0c0e0d0g0b1e1f1d1g0r0q1h0s1m0w210l220z0x33a5353q36100ya73p370i1138271q39280fa80h3a0t0j3b2v3c0va92baa1v3dab0p3e2w3f1wac292r3g2a3h0kas2d3iaradae3k3j2c3l3n3m2h3o342eaf3r1725ag3u3t193vah263s3wai3x12aj4q3y40413z42431i4445ak47am464bal2t48an494aao4c4gap4daqawav4e4f4h2saxa6ay4t4i4u4lazb24jatb04vaub34k4m4w4r4nb1b40u1pb54o2f14b64x4s4p1abs4z4yb7b81j2gb91bba5052bbbd51bc1n53be54551kbi1l32bf5616bvbg572ibj1c18bwbh58bnbkbx59bl5abtbubm15by5hbpbobq5k5l1r5mbz13br5ic01s5n5q5w5j5tc12n2p2l5o315b5r5cc2c45dc3c55s5p5u5vc7c65x5yc8a4c9cd5zca2o1ocb60626164632j1tcccecj1uco65cmckcvcpcnclcf2q1xcycscwcqcxcrczd0ct1y2m5e2kcu5fd16c68d3d4d76d695g66d2d56a676b6e6f6g2u6i6j6kcgch6h6l6mci6o6n706p7172736q6r6sd8d9dc6u6tdedadddf6vdbd66w6xdgdi6ydj6zdhdk76dl77dmdn7a7b747879do7cdpdqdr7d7f7l7i7g7mdt7jdu7e7n7h7kdvdwdxdy7oe2e37pdsdze07r7qe5e1e6e87ued75e47s7te9ebe7eeecekefeaenehelegemeoeiepejeqeres7v817z82807w7x7y838485878889868a8bet8d8c8r8e8s8u8teuevew8f8gex8heyf18j8if2f3f48kezf08lf5f68mf9f78nfa8ofb8xfcf8fd91fffe928y8vfg8zfi8w909996fh9c93fj9a9bflfk97fmfn949d9598fofp9eftfq9i9h9f9gfzfug49k9lfwfv9jg1g2g8fxg0gbg9g3g5gcgegag6gdgffyg7gggkgh8p8q9qfrfs9ogj9r9sgi9p9mgn9t9ngm9ugl9v9w9y9za0a2a19xa3gugvgqgogpgrgsgtgwgxgyh0h1h4h3h2gzh5"
-ON_V = "283p3q5i788y8z95ebej"
+ORDER = "070j0o27010800030k09280q0p0r1q0n1h0l0b0m0s261j0w1k0y060x0t160z028729882b190u89250a101a1r0c2a2c0e0f1x201f8a2d3q1i1n2e2f8b9p8c049o3r8d2g8e2h1g0g158f2i8g171z181y1c1d2j110v2k9r2o050i8h1e2l1l3t138i9s2m2p8j1m8m3u2n123v8n0d2q3w8k0h9t2t2r8l142u2s1o2z2w8o303x8p2v8r318q2x1s8s9u1p9q321b2y8x8u8t8y338z8v34908w3591363738923b399v3a933c9495213d963e3g97993h3f1t9a983i239b3l3j9c3m229e3s3k9d1u9f9j3n9g3o3p9h9k3y9i403z9l44411v429m9n45434a461w47489w494b9y4f9xa2a04ha1a34c4o9za84ka44g4d4e4p4la54ia64j4m24a74nad4q4rafae4s4taaaga9abaiacahakajam51al4xanaoap4vaq52ar4w4y4u4zaz50av53axawatb0ayasau5457b158b25559b35ab5b65bb75cb85eb95i5dba5f5g5j56bbbcbd5o5hbgbe5kbhbfbmbi5q5p5lbnbobj5r5m5s5nbk5tbl5ubp5v62605wb4br5ybs63btbubw615x5zc064bvbybxc165bz666b6f67bqc2c3c4c56d6c6e6g6869cbc76a6hcdccc8c9cecac66i6j6lcf6k6mcgcj6nchck6o6pclcmci6q6rcn6s6t6uco6w6vcq74cp6xcucscr6ycvct76d26zcw75d3d4cx7770727178cy79d5cz7b7c7ed77a7f7id97d7j7gd8dc7hdgdd7kdhdadedb7ldfd6didj737m7ndk7o7v7p7r7q7tdl7sdt7wdm7u7xdrdudsdpdqdndo7y817zdvdwe383dx80e2d08285dz86e1dye484d1e0"
+ON_V = "1o2b2l2q405e6r7n7o8d9paoarb3bcc2c5chcq"
 
+f32, bf, i32, u16, u8, x4 = "float32", "bfloat16", "int32", "uint16", "uint8", "float8_e4m3fn_x4"
 BUF = {
-    "fni": (24, "int32", 0), "pi": (16, "int32", 0), "col": (32, "float32", 0), "bits": (8, "float32", 0),
-    "iota1": (CW, "bfloat16", 0), "iotaT": (CW, "float32", 0), "tw0": (CW, "float32", 0),
-    "r16": (64, "bfloat16", 0), "amp": (C, "bfloat16", 0), "r4": (64, "bfloat16", 0), "amp4": (C, "bfloat16", 0),
-    "base": (C, "float32", 0), "locp": (C, "float32", 0), "locq": (C, "float32", 0), "wr": (C, "float32", 0),
-    "rst": (2 * C, "bfloat16", 0), "mrst": (C, "bfloat16", 0), "cc": (C, "float32", 0),
-    "kwin": (CW, "bfloat16", 0), "wsg": (CW, "float32", 0), "wtmp": (C, "float32", 0), "wtmq": (C, "float32", 0), "tab": (192, "float32", 0),
-    "il": (8 * 32, "float32", 0), "cl": (64, "uint16", 0),
-    "half": (512, "bfloat16", 0), "et": (2048, "bfloat16", 0), "ut": (512, "bfloat16", 0), "vt": (512, "bfloat16", 0),
-    "qe": (512, "float8_e4m3fn_x4", 0), "se": (512, "uint8", 0), "qw": (512, "float8_e4m3fn_x4", 0), "sw": (512, "uint8", 0),
-    "qu0": (128, "float8_e4m3fn_x4", 0), "su0": (128, "uint8", 0), "qu": (128, "float8_e4m3fn_x4", 0), "su": (128, "uint8", 0),
-    "qv": (128, "float8_e4m3fn_x4", 0), "sv": (128, "uint8", 0),
-    "qx": (C, "float8_e4m3fn_x4", 1), "sx": (C, "uint8", 1), "qz": (C, "float8_e4m3fn_x4", 1), "sz": (C, "uint8", 1),
-    "qp0": (QW, "float8_e4m3fn_x4", 1), "sp0": (QW, "uint8", 1), "qp1": (QW, "float8_e4m3fn_x4", 1), "sp1": (QW, "uint8", 1),
-    "qp2": (QW, "float8_e4m3fn_x4", 1), "sp2": (QW, "uint8", 1),
-    "xt": (XW, "bfloat16", 1), "xh": (4 * C, "bfloat16", 1), "xg": (4 * C, "bfloat16", 1), "zt": (4 * C, "bfloat16", 1), "z32": (4 * C, "bfloat16", 1),
-    "y32": (4 * CW, "bfloat16", 1), "pt": (512, "bfloat16", 1), "ph": (4 * SL, "bfloat16", 1), "hf": (4 * SL, "bfloat16", 1),
-    "al": (10 * LW, "uint16", 1), "ar": (5 * CW, "bfloat16", 1), "sb": (C, "bfloat16", 1), "sc": (C, "float32", 1),
-    "flf": (32, "float32", 1), "a5": (C, "bfloat16", 1), "eq": (2 * C, "bfloat16", 1), "eqs": (2 * C, "bfloat16", 1),
-    "sm": (8 * 32, "float32", 1), "smi": (64, "int32", 1), "ov": (LW, "uint16", 1),
-    "fp": (CW, "float32", 1), "vw": (CW, "bfloat16", 1), "keep": (C, "bfloat16", 1), "val": (C, "bfloat16", 1),
-    "hb": (CW, "bfloat16", 1), "gg": (C, "float32", 1),
-    "tt": (5 * CW, "float32", 1), "tw": (CW, "float32", 1),
-    "mx": (C, "float32", 1), "junk": (C, "bfloat16", 1), "hc": (8, "float32", 1), "hl": (2, "uint16", 1),
-    "pl": (32, "uint16", 1), "o2": (LW, "uint16", 1), "fl": (C // 4, "uint16", 1), "gl": (LW, "uint16", 1), "sl": (16, "uint16", 1),
-    "w2": (W2W, "bfloat16", 1), "wg": (C, "float32", 1), "fr": (C, "bfloat16", 1), "fot": (C, "float32", 1), "yo": (C, "float32", 1),
+    "fni": (24, i32, 0), "pi": (16, i32, 0), "col": (32, f32, 0), "tmp": (64, f32, 0),
+    "iotaR": (CW, bf, 0), "iotaT": (CW, f32, 0), "tw0": (CW, f32, 0), "r16": (C, bf, 0), "r4": (C, bf, 0), "loc": (C, bf, 0), "base": (C, bf, 0),
+    "amp": (C, bf, 0), "amp4": (C, bf, 0), "rst": (C, bf, 0), "rmin": (C, bf, 0), "cc": (C, bf, 0),
+    "d0": (192, bf, 0), "d1": (192, bf, 0), "d2": (192, bf, 0), "d3": (192, bf, 0), "d4": (192, bf, 0),
+    "tbl": (C, bf, 0), "ws0": (CW, bf, 0), "ws1": (CW, bf, 0), "kw": (32, bf, 0), "fix": (16, bf, 0),
+    "il": (6 * 16, f32, 0), "li": (16, i32, 0), "cl": (32, u16, 0),
+    "zero": (512, bf, 0), "et": (2048, bf, 0), "ut": (512, bf, 0), "vt": (512, bf, 0),
+    "qe": (512, x4, 0), "se": (512, u8, 0), "qw": (512, x4, 0), "sw": (512, u8, 0),
+    "qu0": (128, x4, 0), "su0": (128, u8, 0), "qu": (128, x4, 0), "su": (128, u8, 0), "qv": (128, x4, 0), "sv": (128, u8, 0),
+    "qx": (C, x4, 1), "sx": (C, u8, 1), "qz": (C, x4, 1), "sz": (C, u8, 1),
+    "qp0": (QW, x4, 1), "sp0": (QW, u8, 1), "qp1": (QW, x4, 1), "sp1": (QW, u8, 1), "qp2": (QW, x4, 1), "sp2": (QW, u8, 1),
+    "xt": (XW, bf, 1), "xh": (4 * C, bf, 1), "xg": (4 * C, bf, 1), "zt": (4 * C, bf, 1), "z32": (4 * C, bf, 1),
+    "y32": (XW, bf, 1), "pt": (512, bf, 1), "ph": (4 * SL, bf, 1), "hf": (4 * SL, bf, 1),
+    "al": (10 * 16, u16, 1), "ar": (8 * CW, bf, 1), "sb": (C, bf, 1), "s4": (C, bf, 1), "wa": (3 * C, bf, 1), "sc": (2 * C, bf, 1),
+    "sm": (8 * 16, f32, 1), "cf": (16, u16, 1), "pos": (16, u16, 1), "kv": (2 * C, bf, 1), "nx": (C, bf, 1),
+    "tt": (5 * CW, f32, 1), "tw": (CW, f32, 1),
+    "mx": (C, f32, 1), "junk": (C, bf, 1), "hc": (8, f32, 1), "hl": (2, u16, 1),
+    "pl": (16, u16, 1), "o2": (16, u16, 1), "fl": (C // 4, u16, 1), "sl": (16, u16, 1),
+    "w2": (W2W, bf, 1), "wg": (2 * C, bf, 1), "fr": (C, bf, 1), "fot": (C, f32, 1), "yo": (C, f32, 1),
 }
 SCRATCH = {k: ("sbuf", [128, v[0] * (NS if v[2] else 1)], v[1]) for k, v in BUF.items()}
-SCRATCH["ps"] = ("psum", [128, 4096], "float32")
+SCRATCH["ps"] = ("psum", [128, 4096], f32)
+SIZE = {f32: 4, bf: 2, i32: 4, u16: 2, u8: 1, x4: 4}
 LOADS = ["fn", "u", "v", "wc", "ws"] + ["x%d" % s for s in range(NS)]
 SEMAPHORES = ["cV", "cS", "cP", "cG", "sent", "stored"] + ["ld_" + k for k in LOADS] + ["dup%d" % s for s in range(NS)] + \
     ["arr%d_%d" % (r, s) for r in range(3) for s in range(NS)]
@@ -59,309 +55,292 @@ SEMAPHORES = ["cV", "cS", "cP", "cG", "sent", "stored"] + ["ld_" + k for k in LO
 def build(g, T, topo, core, rank):
     ops = []
 
-    def reg(name, s, a=0, b=None, step=1):
+    def reg(name, s=0, a=0, b=None, step=1):
         w, _, per = BUF[name]
         o = s * w if per else 0
-        b = w if b is None else b
-        return T[name][:, o + a:o + b:step] if step != 1 else T[name][:, o + a:o + b]
+        return (name, o + a, o + (w if b is None else b), step)
 
-    def add(alts, r, w, s=None, lat=0.0, sem=None, inc=1, arr=None):
-        ops.append({"alts": alts, "r": list(r), "w": list(w), "s": s, "lat": lat, "sem": sem, "inc": inc, "arr": arr})
+    def ap(v):
+        if not isinstance(v, tuple):
+            return v
+        if v[0] == "ind":
+            return ap(v[1]).indirect(ap(v[2]))
+        name, a, b, st = v
+        if st == 1:
+            return T[name][:, a:b]
+        if st < 0:
+            return T[name][:, slice(b - 1, a - 1 if a else None, -1)]
+        return T[name][:, a:b:st]
 
-    def cv(n):
-        return max(64.0, float(n))
+    def ind(win, off):
+        return ("ind", win, off)
 
-    def ts(out, in0, s1, op0, r, w, n, s=None, s2=None, op1=None, gather=False):
-        c = 50 + 1.56 * n if gather else cv(n)
+    def flat(vs):
+        out = []
+        for v in vs:
+            if isinstance(v, tuple):
+                out += [v[1], v[2]] if v[0] == "ind" else [v]
+        return out
+
+    def add(alts, r, w, sem=None, inc=1, arr=None, after=None, dma=False):
+        r, w = flat(r), flat(w)
+        w = w + [v for v in r if v[0] == "ps"]
+        ops.append({"alts": alts, "r": r, "w": w, "sem": sem, "inc": inc, "arr": arr, "after": after, "dma": dma})
+        return len(ops) - 1
+
+    def ts(out, in0, s1, op0, s2=None, op1=None):
         if op1 is None:
-            add({"V": (c, lambda: g.vector.tensor_scalar(out, in0, s1, None, op0))}, r, w, s)
+            add({"V": lambda: g.vector.tensor_scalar(ap(out), ap(in0), ap(s1), None, op0)}, [in0, s1], [out])
         else:
-            add({"V": (c, lambda: g.vector.tensor_scalar(out, in0, s1, s2, op0, op1))}, r, w, s)
+            add({"V": lambda: g.vector.tensor_scalar(ap(out), ap(in0), ap(s1), ap(s2), op0, op1)}, [in0, s1, s2], [out])
 
-    def tt(out, in0, in1, op, r, w, n, s=None, gather=False, psum=False):
-        c = 50 + 1.7 * n if gather else cv(n if psum else 2 * n)
-        add({"V": (c, lambda: g.vector.tensor_tensor(out, in0, in1, op))}, r, w, s)
+    def tt(out, in0, in1, op):
+        add({"V": lambda: g.vector.tensor_tensor(ap(out), ap(in0), ap(in1), op)}, [in0, in1], [out])
 
-    def cp(out, in_, r, w, n, s=None):
-        add({"V": (cv(n), lambda: g.vector.tensor_copy(out, in_))}, r, w, s)
+    def cp(out, in_):
+        add({"V": lambda: g.vector.tensor_copy(ap(out), ap(in_))}, [in_], [out])
 
-    def ms(out, v, w, n, s=None):
-        add({"V": (cv(n), lambda: g.vector.memset(out, v))}, [], w, s)
+    def ms(out, v):
+        add({"V": lambda: g.vector.memset(ap(out), v)}, [], [out])
 
-    def scan(out, d0, d1, init, op0, op1, r, w, n, s=None):
-        add({"V": (cv(n), lambda: g.vector.tensor_tensor_scan(out, d0, d1, init, op0, op1))}, r, w, s)
+    def red(out, in_, op):
+        add({"V": lambda: g.vector.tensor_reduce(ap(out), ap(in_), AxisListType.X, op)}, [in_], [out])
 
-    def gat(out, win, off, r, w, n, s=None, scale=None):
-        src = win.indirect(off)
-        if scale is None:
-            add({"V": (50 + 1.56 * n, lambda: g.vector.tensor_copy(out, src)),
-                 "S": (65 + 1.56 * n, lambda: g.scalar.activation(out, src, F.Copy))}, r, w, s)
+    def scan(out, d0, d1, init, op0, op1):
+        add({"V": lambda: g.vector.tensor_tensor_scan(ap(out), ap(d0), ap(d1), init, op0, op1)}, [d0, d1], [out])
+
+    def copy(out, in_):
+        add({"V": lambda: g.vector.tensor_copy(ap(out), ap(in_)), "S": lambda: g.scalar.activation(ap(out), ap(in_), F.Copy)}, [in_], [out])
+
+    def gat(out, win, off):
+        copy(out, ind(win, off))
+
+    def lin(out, in_, k, c=None):
+        if c is None:
+            add({"V": lambda: g.vector.tensor_scalar(ap(out), ap(in_), ap(k), None, A.mult),
+                 "S": lambda: g.scalar.activation(ap(out), ap(in_), F.Identity, scale=ap(k))}, [in_, k], [out])
         else:
-            add({"V": (50 + 1.56 * n, lambda: g.vector.tensor_scalar(out, src, scale, None, A.mult)),
-                 "S": (65 + 1.56 * n, lambda: g.scalar.activation(out, src, F.Identity, scale=scale))}, r, w, s)
+            add({"V": lambda: g.vector.tensor_scalar(ap(out), ap(in_), ap(k), ap(c), A.mult, A.add),
+                 "S": lambda: g.scalar.activation(ap(out), ap(in_), F.Identity, scale=ap(k), bias=ap(c))}, [in_, k, c], [out])
 
-    def mul(out, in_, k, r, w, n, s=None, fast=True):
-        add({"V": (cv(n / 2 if fast else n), lambda: g.vector.tensor_scalar(out, in_, k, None, A.mult)),
-             "S": (cv(n) + 30, lambda: g.scalar.activation(out, in_, F.Identity, scale=k))}, r, w, s)
+    def quant(q, sc, in_):
+        add({"V": lambda: g.vector.quantize_mx(ap(q), ap(sc), ap(in_))}, [in_], [q, sc])
 
-    def addc(out, in_, colv, r, w, n, s=None):
-        add({"V": (cv(n), lambda: g.vector.tensor_scalar(out, in_, colv, None, A.add)),
-             "S": (cv(n) + 30, lambda: g.scalar.activation(out, in_, F.Identity, bias=colv))}, r, w, s)
+    def mm(out, lq, ls, rq, rs, arr=None, after=None):
+        add({"P": lambda: g.tensor.matmul_mx(ap(out), ap(lq), ap(ls), ap(rq), ap(rs), True, True)}, [lq, ls, rq, rs], [out], arr=arr, after=after)
 
-    def quant(q, sc, in_, r, w, n, s=None):
-        add({"V": (15 + 0.25 * 4 * n, lambda: g.vector.quantize_mx(q, sc, in_))}, r, w, s)
-
-    def mm(out, lq, ls, rq, rs, r, w, n, s=None, arr=None):
-        add({"P": ((n + 16) * 0.9, lambda: g.tensor.matmul_mx(out, lq, ls, rq, rs, True, True))}, r, w, s, arr=arr)
-
-    def iota(out, pat, base, cm, w, n, flt=True):
-        if flt:
-            add({"G": (130 + 2 * n, lambda: g.iota(out, pat, base, cm, allow_small_or_imprecise_dtypes=True))}, [], w)
+    def iota(out, pat, base, cm=0):
+        if BUF[out[0]][1] == i32:
+            add({"G": lambda: g.iota(ap(out), pat, base, cm)}, [], [out])
         else:
-            add({"G": (130 + 2 * n, lambda: g.iota(out, pat, base, cm))}, [], w)
+            add({"G": lambda: g.iota(ap(out), pat, base, cm, allow_small_or_imprecise_dtypes=True)}, [], [out])
 
-    def dma(q, out, in_, r, w, sem, lat, s=None):
+    def sel(out, in_, pat, op, fill, base, cm):
+        add({"G": lambda: g.affine_select(ap(out), ap(in_), pat, op, fill, base, cm)}, [in_], [out])
+
+    def dma(q, out, in_, r, w, sem):
         e = g.sync if q == "Y" else g.scalar
-        add({q: (60.0, lambda: e.dma_start(out, in_))}, r, w, s, lat=lat, sem=sem, inc=16)
+        add({q: lambda: e.dma_start(out, in_)}, r, w, sem=sem, inc=16, dma=True)
 
-    def col(k):
-        return T.col[:, k:k + 1]
+    def col(k, n=1):
+        return ("col", k, k + n, 1)
 
-    def il(m, a=0, b=32, step=1):
-        return T.il[:, 32 * m + a:32 * m + b:step] if step != 1 else T.il[:, 32 * m + a:32 * m + b]
+    def pi(k, n=1):
+        return ("pi", k, k + n, 1)
 
-    def bank(s, t):
+    def il(m, a=0, step=1):
+        return ("il", 16 * m + a, 16 * m + LW, step)
+
+    def bank(s, t, a, b):
         k = s * NB + t % NB
-        return k * 512, "ps%d" % k
+        return ("ps", k * 512 + a, k * 512 + b, 1)
 
-    dma("Y", T.fni[:], T.fn[:], [], ["fni"], "ld_fn", 2000)
-    dma("S", T.ut[:], T.u[:], [], ["ut"], "ld_u", 2200)
+    dma("Y", T.fni[:], T.fn[:], [], [reg("fni")], "ld_fn")
     for s in range(NS):
-        dma("Y" if s % 2 == 0 else "S", reg("xt", s, 0, 4 * C), T.x[:, 4 * C * s:4 * C * (s + 1)], [], ["xt%d" % s], "ld_x%d" % s, 2800, s)
-    dma("Y", T.qw[:].bitcast(dt.uint8), T.wc[:], [], ["qw"], "ld_wc", 3000)
-    dma("Y", T.sw[:], T.ws[:], [], ["sw"], "ld_ws", 2500)
-    dma("Y", T.vt[:], T.v[:], [], ["vt"], "ld_v", 2500)
+        v = reg("xt", s, 0, 4 * C)
+        dma("S" if s % 2 == 0 else "Y", ap(v), T.x[:, 4 * C * s:4 * C * (s + 1)], [], [v], "ld_x%d" % s)
+    dma("S", T.ut[:], T.u[:], [], [reg("ut")], "ld_u")
+    dma("Y", T.qw[:].bitcast(dt.uint8), T.wc[:], [], [reg("qw")], "ld_wc")
+    dma("Y", T.sw[:], T.ws[:], [], [reg("sw")], "ld_ws")
+    dma("Y", T.vt[:], T.v[:], [], [reg("vt")], "ld_v")
 
-    iota(T.pi[:, 0:1], [[0, 1]], 0, 1, ["pi0"], 1, False)
-    iota(T.r16[:, 0:16], [[1, 16]], 0, 0, ["r16"], 16)
-    iota(T.iota1[:, 0:C], [[1, C]], 1, 0, ["iota1"], C)
-    iota(il(0), [[16, 32]], 0, 0, ["il0"], 32)
-    iota(T.base[:], [[32, B], [0, 32]], 0, 0, ["base"], C)
-    iota(T.locp[:], [[0, H], [32, 2], [1, 32]], 1, 0, ["locp"], C)
-    iota(T.locq[:], [[0, H], [-32768, 2], [1, 32]], 1, 0, ["locq"], C)
-    iota(il(3), [[32, 16], [0, 2]], -1, 0, ["il3"], 32)
-    iota(il(5), [[0, 16], [16, 2]], 0, 0, ["il5"], 32)
-    iota(T.iotaT[:, 0:C], [[1, C]], 0, 0, ["iotaT"], C)
-    iota(T.r4[:, 0:16], [[0, 4], [1, 4]], 0, 0, ["r4"], 16)
-    iota(T.wr[:], [[32, B], [0, 32]], 32 + C, 0, ["wr"], C)
-    iota(il(6, 0, 16), [[0, 8], [1, 2]], 0, 0, ["il6"], 16)
-    iota(il(7, 0, 4 * H), [[1, 4], [0, H]], 0, 0, ["il7"], 16)
-    ms(T.iota1[:, C:CW], float(C + 1), ["iotap"], 16)
-    ts(T.pi[:, 1:2], T.pi[:, 0:1], 15, A.bitwise_and, ["pi0"], ["pi1"], 1)
-    pj = T.pi[:, 1:2]
-    cp(col(0), pj, ["pi1"], ["c0"], 1)
-    ts(col(1), pj, 1.0, A.add, ["pi1"], ["c1"], 1)
-    ts(col(2), pj, 16.0, A.add, ["pi1"], ["c2"], 1)
-    ts(col(3), pj, 17.0, A.add, ["pi1"], ["c3"], 1)
-    ts(col(20), pj, 15.0, A.is_equal, ["pi1"], ["c20"], 1, s2=255.0, op1=A.mult)
-    ts(col(4), col(20), 1.0, A.add, ["c20"], ["c4"], 1, s2=1.0 / 256, op1=A.mult)
-    ts(col(5), pj, float(B - 1), A.min, ["pi1"], ["c5"], 1, s2=32.0, op1=A.mult)
-    ts(col(6), col(5), -1.0, A.mult, ["c5"], ["c6"], 1, s2=float(C - 32), op1=A.add)
-    ts(col(7), pj, 1.0, A.add, ["pi1"], ["c7"], 1, s2=-1024.0, op1=A.mult)
-    ts(col(8), pj, 17.0, A.add, ["pi1"], ["c8"], 1, s2=-1024.0, op1=A.mult)
+    iota(pi(0), [[0, 1]], 0, 1)
+    iota(reg("iotaR", 0, 0, C), [[1, C]], RO)
+    iota(reg("r16"), [[0, C // 16], [1, 16]], 0)
+    iota(reg("loc"), [[0, B], [1, 32]], 0)
+    iota(("li", 0, LW, 1), [[0, B], [16, 2]], 0, 1)
+    iota(il(0), [[16, LW]], 0)
+    iota(reg("iotaT", 0, 0, C), [[1, C]], 0)
+    iota(reg("base"), [[32, B], [0, 32]], 0)
+    iota(reg("r4"), [[0, C // 4], [1, 4]], 0)
+    iota(("kw", 0, 2, 1), [[-1, 2]], 1)
+    iota(("kw", 16, 18, 1), [[1, 2]], 0)
+    iota(("fix", 0, LW, 1), [[C + RO, 2], [0, B]], 0)
+    ts(pi(1), pi(0), 15, A.bitwise_and)
+    ts(pi(2), pi(0), 2, A.logical_shift_right, 3, A.bitwise_and)
+    ts(pi(3), pi(0), 3, A.bitwise_and)
+    ts(pi(4), pi(0), 1, A.logical_shift_right, 7, A.bitwise_and)
     for m in range(4):
-        ts(T.pi[:, 4 + m:5 + m], T.pi[:, 0:1], m, A.logical_shift_right, ["pi0"], ["pb%d" % m], 1, s2=1, op1=A.bitwise_and)
-    pb = ["pb%d" % m for m in range(4)]
-    ts(T.col[:, 12:16], T.pi[:, 4:8], 5120.0, A.mult, pb, ["c12"], 4, s2=-4096.0, op1=A.add)
-    ts(T.bits[:, 4:8], T.pi[:, 4:8], 1024.0, A.mult, pb, ["bitk"], 4)
-    add({"V": (64.0, lambda: g.vector.tensor_reduce(col(9), T.bits[:, 4:7], AxisListType.X, A.add))}, ["bitk"], ["c9"])
-    add({"V": (64.0, lambda: g.vector.tensor_reduce(col(10), T.bits[:, 4:8], AxisListType.X, A.add))}, ["bitk"], ["c10"])
-    cp(col(11), T.pi[:, 7:8], pb, ["c11"], 1)
-    ts(T.pi[:, 2:3], T.pi[:, 0:1], 3, A.bitwise_and, ["pi0"], ["pi2"], 1)
-    ts(T.pi[:, 3:4], T.pi[:, 0:1], 2, A.logical_shift_right, ["pi0"], ["pi3"], 1, s2=3, op1=A.bitwise_and)
-    ts(col(17), T.pi[:, 2:3], -4.0, A.add, ["pi2"], ["c17"], 1)
-    cp(col(18), T.pi[:, 3:4], ["pi3"], ["c18"], 1)
-    ts(col(19), T.pi[:, 3:4], 1.0, A.add, ["pi3"], ["c19"], 1)
-    ts(col(21), T.pi[:, 3:4], 3.0, A.is_equal, ["pi3"], ["c21"], 1, s2=255.0, op1=A.mult)
-    ts(col(16), col(21), 1.0, A.add, ["c21"], ["c16"], 1, s2=4.0 / 256, op1=A.mult)
-    ts(T.cl[:, 44:44 + 2 * B], il(0, 0, 2 * B), 0.0, A.mult, ["il0", "c0"], ["cl3"], 2 * B, s2=col(0), op1=A.add)
-    for nm, src, c0 in (("amp", "r16", 0), ("amp4", "r4", 18)):
-        w = T[src]
-        ts(w[:, 16:32], w[:, 0:16], col(c0), A.not_equal, [src, "c%d" % c0], [src + "a"], 16)
-        ts(w[:, 32:48], w[:, 0:16], col(c0 + 1), A.is_equal, [src, "c%d" % (c0 + 1)], [src + "b"], 16, s2=255.0, op1=A.mult)
-        tt(w[:, 48:64], w[:, 16:32], w[:, 32:48], A.add, [src + "a", src + "b"], [src + "c"], 16)
-        gat(T[nm][:], w[:, 48:64], T.cl[:, 44:44 + 2 * B], [src + "c", "cl3"], [nm], C)
-    ts(il(1), il(0), col(1), A.add, ["il0", "c1"], ["il1"], 32)
-    ts(il(2), il(0), col(0), A.add, ["il0", "c0"], ["il2"], 32, s2=32.0, op1=A.add)
-    ts(il(4), il(0), col(0), A.add, ["il0", "c0"], ["il4"], 32, s2=float(C), op1=A.add)
-    ts(T.cl[:, 0:32], il(5), col(0), A.add, ["il5", "c0"], ["cl0"], 32)
-    cp(T.cl[:, 32:40], il(0, 0, 8), ["il0"], ["cl1"], 8)
-    ts(il(6, 16, 32), il(6, 0, 16), col(11), A.not_equal, ["il6", "c11"], ["il6b"], 16, s2=-4096.0, op1=A.mult)
-    ts(il(6, 0, 16), il(6, 16, 32), col(9), A.subtract, ["il6b", "c9"], ["il6"], 16)
-    ms(il(7, 16, 32), 0.0, ["il7b"], 16)
-    ts(il(7, 16, 16 + 4 * H), il(7, 0, 4 * H), 0.25, A.mult, ["il7"], ["il7b"], 16)
-    ts(T.tab[:, 0:16], T.r16[:, 0:16], col(0), A.is_le, ["r16", "c0"], ["tab0"], 16)
-    add({"V": (64.0, lambda: g.vector.tensor_reduce(col(22), T.tab[:, H:16:H], AxisListType.X, A.add))}, ["tab0"], ["c22"])
-    ts(col(23), col(22), float(-H), A.mult, ["c22", "c0"], ["c23"], 1, s2=col(0), op1=A.add)
-    cp(T.cl[:, 40:41], col(23), ["c23"], ["cl2"], 1)
-    ms(T.rst[:], 1.0, ["rst"], C)
-    ms(T.rst[:, 0:2 * C:32], 0.0, ["rst"], 2 * B)
-    ms(T.mrst[:], 0.0, ["mrst"], C / 2)
-    ms(T.mrst[:, 0:C:32], 2.0 ** 20, ["mrst"], B)
-    ms(T.kwin[:], 0.0, ["kwin"], CW / 2)
-    ms(T.kwin[:, 0:1], 1.0, ["kwin"], 1)
-    ts(T.wtmq[:], T.base[:], col(5), A.is_equal, ["base", "c5"], ["wtmq"], C, s2=-0.5, op1=A.add)
-    mul(T.cc[:], T.wtmq[:], 2 * BIG, ["wtmq"], ["cc"], C, fast=False)
-    ms(T.iotaT[:, C:CW], TSINK, ["iotaTp"], 16)
-    addc(T.tw0[:], T.iotaT[:], col(12), ["iotaT", "iotaTp", "c12"], ["tw0"], CW)
-    lo = T.locp[:, 0:32]
-    ts(T.tab[:, 0:32], lo, col(0), A.is_le, ["locp", "c0"], ["tab0"], 32)
-    ts(T.tab[:, 32:64], lo, col(2), A.is_le, ["locp", "c2"], ["tab1"], 32, s2=1024.0, op1=A.mult)
-    ts(T.tab[:, 64:96], lo, col(1), A.is_equal, ["locp", "c1"], ["tab2"], 32)
-    ts(T.tab[:, 96:128], lo, col(3), A.is_equal, ["locp", "c3"], ["tab3"], 32, s2=1024.0, op1=A.mult)
-    tt(T.tab[:, 128:160], T.tab[:, 0:32], T.tab[:, 32:64], A.add, ["tab0", "tab1"], ["tab4"], 32)
-    tt(T.tab[:, 160:192], T.tab[:, 64:96], T.tab[:, 96:128], A.add, ["tab2", "tab3"], ["tab5"], 32)
-    tt(T.wtmp[:], T.tab[:, 160:192].indirect(T.cl[:, 0:2 * B]), T.wr[:], A.mult, ["tab5", "cl0", "wr"], ["wtmp"], C, gather=True)
-    tt(T.wsg[:, 0:C], T.tab[:, 128:160].indirect(T.cl[:, 0:2 * B]), T.wtmp[:], A.add, ["tab4", "cl0", "wtmp"], ["wsg"], C, gather=True)
-    ms(T.wsg[:, C:CW], 0.0, ["wsgp"], 16)
-    ms(T.half[:], 0.5, ["half"], 256)
+        ts(pi(5 + m), pi(0), m, A.logical_shift_right, 1, A.bitwise_and)
+    cp(col(0), pi(1))
+    cp(col(1, 7), pi(2, 7))
+    ts(col(8, 4), col(4, 4), 1024.0, A.mult)
+    red(col(12), col(8, 4), A.add)
+    ts(col(13), col(2), -4.0 * RO, A.add)
+    ts(col(14), col(3), float(B - 1), A.min, 32.0, A.mult)
+    ts(col(15), col(4), float(CW), A.mult, col(14), A.add)
+    ts(reg("amp"), reg("r16"), col(0), A.is_gt, 16.0, A.mult)
+    ts(("tmp", 0, 16, 1), reg("r16", 0, 0, 16), col(0), A.is_le, 0.0625, A.max)
+    red(col(16), ("tmp", 0, 16, 1), A.mult)
+    ts(reg("amp4"), reg("r4"), col(1), A.is_gt, 16.0, A.mult)
+    ts(("tmp", 16, 20, 1), reg("r4", 0, 0, 4), col(1), A.is_le, 0.0625, A.max)
+    iota(("tmp", 20, 21, 1), [[0, 1]], 4)
+    red(col(17), ("tmp", 16, 21, 1), A.mult)
+    ts(reg("rst"), reg("loc"), 0.0, A.not_equal)
+    ms(reg("rmin"), 1000.0)
+    ts(reg("rmin", 0, 31, C, 32), reg("base", 0, 0, C, 32), float(-SH), A.add)
+    ts(reg("cc"), reg("base"), col(14), A.not_equal, -BIG, A.mult)
+    ms(reg("iotaR", 0, C, CW), 256.0)
+    ms(reg("iotaT", 0, C, CW), TSINK)
+    lin(reg("tw0", 0, 0, C + 1), reg("iotaT", 0, 0, C + 1), col(4), col(8))
+    ts(il(1), il(0), col(0), A.add, float(-SH), A.add)
+    ts(il(2), il(0), col(0), A.add, float(4 * C), A.add)
+    ts(il(3), il(0), col(0), A.add, float(CW), A.add)
+    cp(("cl", 0, LW, 1), ("li", 0, LW, 1))
+    cp(("cl", 16, 24, 1), ("il", 0, 8, 1))
+    iota(reg("zero"), [[0, 512]], 0)
+    iota(reg("d0", 0, 0, 160), [[0, 160]], 1)
+    sel(reg("d1", 0, 0, 144), reg("zero", 0, 0, 144), [[1, 144]], A.not_equal, 1.0, 0, -1)
+    sel(reg("d2", 0, 0, 144), reg("d1", 0, 0, 144), [[1, 144]], A.not_equal, -1.0, -16, -1)
+    sel(reg("d3", 0, 0, 160), reg("d0", 0, 0, 160), [[-1, 160]], A.is_gt, 0.0, 16, 1)
+    sel(reg("d4", 0, 0, 160), reg("d3", 0, 0, 160), [[1, 160]], A.not_equal, float(CW), -16, -1)
+    lc = ("cl", 0, LW, 1)
+    gat(reg("tbl"), reg("d2", 0, 0, 144), lc)
+    gat(reg("ws0", 0, 0, C), reg("d4", 0, 16, 160), lc)
+    gat(reg("ws1", 0, 0, C), reg("d4", 0, 0, 144), lc)
+    ms(reg("ws0", 0, C, CW), 0.0)
+    ms(reg("ws1", 0, C, CW), 0.0)
     for b in range(4):
-        add({"G": (170 + 2 * 512, lambda b=b: g.affine_select(T.et[:, 512 * b:512 * b + 512], T.half[:], [[8, 128], [1, 4]], A.is_equal, 0.0, -b, -8))},
-            ["half"], ["et%d" % b])
-        quant(T.qe[:, 128 * b:128 * b + 128], T.se[:, 128 * b:128 * b + 128], T.et[:, 512 * b:512 * b + 512], ["et%d" % b], ["qe%d" % b], 128)
-    quant(T.qu0[:], T.su0[:], T.ut[:], ["ut"], ["qu0"], 128)
-    add({"V": (250.0, lambda: g.vector.tensor_copy(T.qu[:].bitcast(dt.uint32), T.qu0[:].bitcast(dt.uint32).indirect(T.cl[:, 32:40])))}, ["qu0", "cl1"], ["qu"])
-    add({"S": (265.0, lambda: g.scalar.activation(T.su[:], T.su0[:].indirect(T.cl[:, 32:40]), F.Copy))}, ["qu0", "cl1"], ["su"])
-    quant(T.qv[:], T.sv[:], T.vt[:], ["vt"], ["qv"], 128)
+        sel(("et", 512 * b, 512 * b + 512, 1), reg("zero"), [[8, 128], [1, 4]], A.not_equal, 0.5, -b, -8)
+    quant(reg("qe"), reg("se"), reg("et"))
+    quant(reg("qu0"), reg("su0"), reg("ut"))
+    lu = ("cl", 16, 24, 1)
+    add({"V": lambda: g.vector.tensor_copy(T.qu[:].bitcast(dt.uint32), T.qu0[:].bitcast(dt.uint32).indirect(ap(lu)))}, [reg("qu0"), lu], [reg("qu")])
+    add({"S": lambda: g.scalar.activation(T.su[:], T.su0[:].indirect(ap(lu)), F.Copy)}, [reg("su0"), lu], [reg("su")])
+    quant(reg("qv"), reg("sv"), reg("vt"))
     for s in range(NS):
-        iota(reg("pt", s, 4 * SL, 512), [[0, 512 - 4 * SL]], 0, 0, ["ptz%d" % s], 512 - 4 * SL)
-    ms(T.al[:], C, ["alz"], 5 * LW * NS)
-    ms(T.hb[:, 0:NS * CW:CW], 0.0, ["hb0"], 1)
-    ms(T.vw[:, 0:NS * CW:CW], 0.0, ["vw0"], 1)
-    ms(T.fp[:, 0:NS * CW:CW], 2.0 ** 17, ["fp0"], 1)
-    ms(T.y32[:, C:4 * CW * NS:CW], 0.0, ["yz"], 8)
+        iota(reg("pt", s, 4 * SL, 512), [[0, 512 - 4 * SL]], 0)
+        iota(reg("y32", s, 4 * C, XW), [[0, 4 * SL]], 0)
+    ms(("ar", C, 8 * CW * NS, CW), float(C + RO))
+    ms(("w2", C, W2W * NS, W2W), float(C + RO))
+    ms(("nx", C - 1, C * NS, C), float(C + RO))
+    ms(("tt", C, 5 * CW * NS, CW), TSINK)
 
     def stream(s):
-        def k(name):
-            return "%s%s" % (name, "_%d" % s)
+        def r(name, a=0, b=None, step=1):
+            return reg(name, s, a, b, step)
 
-        def al(m, n=2 * B):
-            return reg("al", s, m * LW, m * LW + n)
+        def al(m):
+            return r("al", m * 16, m * 16 + LW)
 
-        def ar(m, n=CW):
-            return reg("ar", s, m * CW, m * CW + n)
+        def ar(m, n=C):
+            return r("ar", m * CW, m * CW + n)
 
-        def tb(m, n=CW):
-            return reg("tt", s, m * CW, m * CW + n)
+        def tb(m, n=C):
+            return r("tt", m * CW, m * CW + n)
 
-        def sm(m, a=0, b=2 * B, step=1):
-            return reg("sm", s, 32 * m + a, 32 * m + b, step)
+        def sm(m, a=0, step=1):
+            return r("sm", 16 * m + a, 16 * m + LW, step)
 
-        def tolist(out, row, r, w):
-            scan(reg("sb", s), T.amp[:], row, 0.0, A.mult, A.max, r + ["amp"], [k("sb")], C / 2, s)
-            ts(out, reg("sb", s, 15, C, 16), col(4), A.mult, [k("sb"), "c4", "alz"], w, 2 * B, s, s2=-1.0, op1=A.add)
+        def tolist(out, row):
+            scan(r("sb"), reg("amp"), row, 0.0, A.mult, A.max)
+            ts(out, r("sb", 15, C, 16), col(16), A.mult, float(-RO), A.add)
 
-        X = "xt%d" % s
-        ms(reg("w2", s, 0, 32), 1.0, [k("w2p")], 32, s)
-
-        fs = T.fni[:, 2 * B * s:2 * B * (s + 1)]
-        ts(al(0), fs, float(s * C), A.subtract, ["fni", "alz"], [k("al0")], 2 * B, s)
-        ts(reg("flf", s, 0, 2 * B), fs, float(s * C), A.subtract, ["fni"], [k("flf")], 2 * B, s)
-        gat(ar(0, C), T.iota1[:, 0:C], al(0), ["iota1", k("al0")], [k("ar0")], C, s)
+        fs = ("fni", LW * s, LW * (s + 1), 1)
+        par = r("w2", 0, C)
+        ts(al(0), fs, float(s * C), A.subtract)
+        ts(sm(0), fs, float(s * C), A.subtract)
+        gat(par, reg("iotaR", 0, 0, C), al(0))
+        row = par
         for m in range(4):
-            gat(ar(m + 1, C), ar(m, C), al(m), [k("ar%d" % m), k("al%d" % m)], [k("ar%d" % (m + 1))], C, s)
-            tolist(al(m + 1), ar(m + 1, C), [k("ar%d" % (m + 1))], [k("al%d" % (m + 1))])
-        tt(reg("a5", s), ar(4, C).indirect(al(4)), T.base[:], A.subtract, [k("ar4"), k("al4"), "base"], [k("a5")], C, s, gather=True)
+            gat(ar(m), row, al(m))
+            tolist(al(m + 1), ar(m))
+            row = ar(m)
+        gat(r("wa", 0, C), reg("tbl"), al(3))
+        gat(r("wa", C, 2 * C), r("wa", 0, C), al(3))
+        gat(r("wa", 2 * C, 3 * C), r("wa", C, 2 * C), al(4))
+        cf = r("cf", 0, LW)
         for e in range(2):
-            ts(reg("eq", s, e * C, e * C + C), reg("a5", s), col(1 + 2 * e), A.is_equal, [k("a5"), "c%d" % (1 + 2 * e)], [k("eq%d" % e)], C / 2, s)
-        scan(reg("eqs", s), T.rst[:], reg("eq", s), 0.0, A.mult, A.max, ["rst", k("eq0"), k("eq1")], [k("eqs0"), k("eqs1")], C, s)
-        for e in range(2):
-            tt(sm(0, e, 2 * B, 2), reg("eqs", s, e * C + 31, e * C + C, 32), il(1, e, 2 * B, 2), A.mult, [k("eqs%d" % e), "il1"], [k("sm0%d" % e)], B, s)
-        cp(reg("ov", s, 0, 2 * B), sm(0), [k("sm00"), k("sm01")], [k("ov")], 2 * B, s)
-        ov = reg("ov", s, 0, 2 * B)
-        gat(reg("fp", s, 1, C + 1), T.locq[:], al(0), ["locq", k("al0")], [k("fp")], C, s)
-        gat(reg("vw", s, 1, C + 1), T.locp[:], al(0), ["locp", k("al0")], [k("vw")], C, s, scale=1024.0)
-        ts(sm(1), sm(0), 0.0, A.is_gt, [k("sm00"), k("sm01")], [k("sm1")], 2 * B, s, s2=float(C), op1=A.mult)
-        tt(sm(2), sm(1), reg("flf", s, 0, 2 * B), A.max, [k("sm1"), k("flf")], [k("sm2")], 2 * B, s)
-        gat(reg("keep", s), T.kwin[:], ov, ["kwin", k("ov")], [k("keep")], C, s)
-        gat(reg("val", s), reg("vw", s, 0, C + 1), ov, [k("vw"), "vw0", k("ov")], [k("val")], C, s)
-        scan(reg("hb", s, 1, C + 1), reg("keep", s), reg("val", s), 0.0, A.mult, A.add, [k("keep"), k("val")], [k("hb")], C / 2, s)
-        tt(reg("gg", s), reg("fp", s, 0, C + 1).indirect(ov), reg("hb", s, 0, C), A.add, [k("fp"), "fp0", k("ov"), k("hb"), "hb0"], [k("gg")], C, s, gather=True)
-        for e in range(2):
-            o, cb = reg("eq", s, e * C, e * C + C), col(7 + e)
-            add({"S": (C + 30.0, lambda o=o, cb=cb: g.scalar.activation(o, reg("gg", s), F.Abs, bias=cb))}, [k("gg"), "c%d" % (7 + e)], [k("eq%d" % e)], s)
-            scan(reg("eqs", s, e * C, e * C + C), T.mrst[:], o, 0.0, A.max, A.min, ["mrst", k("eq%d" % e)], [k("eqs%d" % e)], C / 2, s)
-            tt(sm(3, e, 2 * B, 2), reg("eqs", s, e * C + 31, e * C + C, 32), il(3, e, 2 * B, 2), A.add, [k("eqs%d" % e), "il3"], [k("sm3%d" % e)], B, s)
-        tt(sm(4), sm(3), sm(2), A.min, [k("sm30"), k("sm31"), k("sm2")], [k("sm4")], 2 * B, s)
-        cp(al(5), sm(4), [k("sm4"), "alz"], [k("al5")], 2 * B, s)
-        n1 = 2 * B + 1
-        par = reg("w2", s, 32, 32 + CW)
-        gat(par, T.iota1[:], al(5, n1), ["iota1", "iotap", k("al5")], [k("w2a"), k("w2b")], CW, s)
+            scan(r("sc", e * C, e * C + C), reg("rst"), r("wa", 2 * C, 3 * C), 0.0, A.mult, A.min if e else A.max)
+            ts(r("cf", e, LW, 2), r("sc", e * C + 31, e * C + C, 32), -1.0 if e else 1.0, A.mult)
+        gat(r("kv", 0, C), ("kw", 0, 2, 1), cf)
+        tt(r("kv", C, 2 * C), ind(("kw", 16, 18, 1), cf), par, A.mult)
+        cp(r("kv", 0, 2 * C, 32), ("fix", 0, LW, 1))
+        scan(r("nx", 0, C - 1, -1), r("kv", 1, C, -1), r("kv", C + 1, 2 * C, -1), float(C + RO), A.mult, A.add)
+        ts(sm(1), cf, 0.0, A.is_equal, 1000.0, A.mult)
+        tt(sm(2), sm(1), sm(0), A.add)
+        tt(sm(3), sm(2), il(3), A.min)
+        cp(r("pos", 0, LW), sm(3))
+        cp(ind(r("w2"), r("pos", 0, LW)), r("nx"))
+        tolist(al(5), par)
+        row = r("w2", 0, C + 1)
         for m in range(4):
-            lk = [k("al%d" % (5 + m))]
+            gat(ar(4 + m), row, al(5 + m))
             if m == 0:
-                gat(ar(1), par, al(5, n1), [k("w2a"), k("w2b")] + lk, [k("ar1")], CW, s)
-                tt(tb(0), T.tw0[:].indirect(al(5, n1)), T.iotaT[:], A.max, ["tw0", "iotaT", "iotaTp"] + lk, [k("tt0")], CW, s, gather=True)
+                tt(tb(0), ind(reg("tw0", 0, 0, C + 1), al(5)), reg("iotaT", 0, 0, C), A.max)
             else:
-                gat(ar(m + 1), ar(m), al(5 + m, n1), [k("ar%d" % m)] + lk, [k("ar%d" % (m + 1))], CW, s)
-                addc(reg("tw", s), tb(m - 1), col(12 + m), [k("tt%d" % (m - 1)), "c12"], [k("tw")], CW, s)
-                tt(tb(m), reg("tw", s).indirect(al(5 + m, n1)), tb(m - 1), A.max, [k("tw"), k("tt%d" % (m - 1))] + lk, [k("tt%d" % m)], CW, s, gather=True)
-            tolist(al(6 + m), ar(m + 1, C), [k("ar%d" % (m + 1))], [k("al%d" % (6 + m))])
-        gat(tb(4, C), tb(3), al(9), [k("tt3"), k("al9")], [k("tt4")], C, s)
+                lin(r("tw", 0, C + 1), tb(m - 1, C + 1), col(4 + m), col(8 + m))
+                tt(tb(m), ind(r("tw", 0, C + 1), al(5 + m)), tb(m - 1), A.max)
+            tolist(al(6 + m), ar(4 + m))
+            row = ar(4 + m, C + 1)
+        gat(tb(4), tb(3, C + 1), al(9))
 
-        qx, sx, qz, sz = reg("qx", s), reg("sx", s), reg("qz", s), reg("sz", s)
+        qx, sx, qz, sz = r("qx"), r("sx"), r("qz"), r("sz")
+        X = r("xt", 0, 4 * C)
         for rd in range(3):
-            quant(qx, sx, reg("xt", s, 0, 4 * C), [X], [k("qx")], C, s)
-            mul(reg("xh", s), reg("xt", s, 0, 4 * C), 0.5, [X], [k("xh")], 4 * C, s)
-            dma("Y", reg("xg", s), reg("xh", s), [k("xh")], [k("xg")], "dup%d" % s, 2500, s)
-            o, bk = bank(s, 0)
-            mm(T.ps[:, o:o + C], T.qu[:], T.su[:], qx, sx, ["qu", "su", k("qx")], [bk], C, s)
-            scan(reg("mx", s), T.ps[:, o:o + C], T.cc[:], -BIG, A.max, A.min, ["cc"], [bk, k("mx")], C, s)
-            add({"V": (64.0, lambda: g.vector.tensor_reduce(reg("hc", s, 0, 1), reg("mx", s, 31, C, 32), AxisListType.X, A.max))}, [k("mx")], [k("hc0")], s)
-            add({"S": (C + 50.0, lambda: g.scalar.activation(reg("junk", s), reg("mx", s), F.Sign, bias=reg("hc", s, 0, 1), scale=-1.0, accum_out=reg("hc", s, 4, 5)))},
-                [k("mx"), k("hc0")], [k("junk"), k("hc1")], s)
-            ts(reg("hl", s, 0, 1), reg("hc", s, 4, 5), col(6), A.subtract, [k("hc1"), "c6"], [k("hl")], 1, s)
-            hl = reg("hl", s, 0, 1)
+            quant(qx, sx, X)
+            lin(r("xh"), X, 0.5)
+            dma("Y", ap(r("xg")), ap(r("xh")), [r("xh")], [r("xg")], "dup%d" % s)
+            o = bank(s, 0, 0, C)
+            mm(o, reg("qu"), reg("su"), qx, sx)
+            scan(r("mx"), o, reg("cc"), -BIG, A.max, A.add)
+            red(r("hc", 0, 1), r("mx", 31, C, 32), A.max)
+            add({"S": lambda: g.scalar.activation(ap(r("junk")), ap(r("mx")), F.Sign, bias=ap(r("hc", 0, 1)), scale=-1.0, accum_out=ap(r("hc", 4, 5)))},
+                [r("mx"), r("hc", 0, 1)], [r("junk"), r("hc", 4, 5)])
+            hl = r("hl", 0, 1)
+            ts(hl, r("hc", 4, 5), col(15), A.add, float(32 - C), A.add)
+            ts(r("pl"), ind(r("tt", 3 * CW, 5 * CW - 16), hl), col(12), A.subtract, float(C), A.min)
+            pl = r("pl", 0, LW)
+            path = r("w2", CW, W2W)
             for e in range(2):
-                ts(reg("pl", s, e, 32, 2), tb(3 + e, C).indirect(hl), col(10), A.subtract, [k("tt%d" % (3 + e)), k("hl"), "c10"], [k("pl%d" % e)], 16, s,
-                   s2=float(C), op1=A.min, gather=True)
-            pl = reg("pl", s, 0, 2 * B)
-            pk = [k("pl0"), k("pl1")]
-            gat(reg("wg", s), T.wsg[:], pl, ["wsg", "wsgp"] + pk, [k("wg")], C, s)
-            gat(reg("w2", s, 32 + C, W2W), T.iota1[:], pl, ["iota1", "iotap"] + pk, [k("w2b")], C, s)
-            scan(reg("sc", s), T.rst[:, 0:C], reg("wg", s), 0.0, A.mult, A.add, ["rst", k("wg")], [k("sc")], C, s)
-            cp(reg("smi", s, 0, B), reg("sc", s, 31, C, 32), [k("sc")], [k("si")], B, s)
-            ts(reg("smi", s, 32, 32 + 2 * B, 2), reg("smi", s, 0, B), 1023, A.bitwise_and, [k("si")], [k("q0")], B, s)
-            ts(reg("smi", s, 33, 32 + 2 * B, 2), reg("smi", s, 0, B), 10, A.logical_shift_right, [k("si")], [k("q1")], B, s)
-            tt(sm(5), reg("smi", s, 32, 32 + 2 * B), il(2, 0, 2 * B), A.max, [k("q0"), k("q1"), "il2"], [k("sm5")], 2 * B, s)
-            cp(reg("o2", s, 0, 2 * B), sm(5), [k("sm5")], [k("o2")], 2 * B, s)
-            gat(reg("fr", s), reg("w2", s), reg("o2", s, 0, 2 * B), [k("w2p"), k("w2a"), k("w2b"), k("o2")], [k("fr")], C, s)
-            scan(reg("sb", s), T.amp4[:], reg("fr", s), 0.0, A.mult, A.max, [k("fr"), "amp4"], [k("sb")], C / 2, s)
-            ts(reg("fl", s), reg("sb", s, 3, C, 4), col(16), A.mult, [k("sb"), "c16", "c17"], [k("fl")], C // 4, s, s2=col(17), op1=A.add)
+                gat(r("wg", e * C, e * C + C), reg("ws%d" % e, 0, 0, C + 1), pl)
+            gat(path, reg("iotaR", 0, 0, C + 1), pl)
+            for e in range(2):
+                scan(r("sc", e * C, e * C + C, -1), reg("rmin", 0, 0, C, -1), r("wg", e * C, e * C + C, -1), 1000.0, A.min, A.add)
+                tt(sm(4, e, 2), r("sc", e * C, e * C + C, 32), il(1, e, 2), A.max)
+            ts(r("o2", 0, LW), sm(4), float(SH), A.add)
+            gat(r("fr"), r("w2"), r("o2", 0, LW))
+            scan(r("sb"), reg("amp4"), r("fr"), 0.0, A.mult, A.max)
+            ts(r("fl"), r("sb", 3, C, 4), col(17), A.mult, col(13), A.add)
             if rd == 2:
-                ts(reg("fot", s), reg("fr", s), float(s * C - 1), A.add, [k("fr")], [k("fot")], C, s)
-                dma("Y", T.fo[:, s * C:s * C + C], T.fot[0:128:16, s * C:s * C + C], [k("fot")], [], "stored", 2000, s)
-            tt(sm(6, 0, 16), tb(2, C).indirect(hl), il(6, 0, 16), A.add, [k("tt2"), k("hl"), "il6"], [k("sm6")], 16, s, gather=True)
-            tt(sm(7, 0, H), sm(6, 0, B, 2), sm(6, 1, B, 2), A.max, [k("sm6")], [k("sm7a")], H, s)
-            ts(reg("gl", s, 0, H), sm(7, 0, H), float(C), A.min, [k("sm7a")], [k("gl")], H, s)
-            tt(sm(7, 8, 8 + H), sm(7, 0, H), il(4, 0, H), A.min, [k("sm7a"), "il4"], [k("sm7b")], H, s)
-            tt(sm(7, 16, 32), sm(7, 8, 8 + H).indirect(T.cl[:, 40:41]), il(7, 16, 32), A.add, [k("sm7b"), "cl2", "il7b"], [k("sm7c")], 16, s, gather=True)
-            ts(reg("sl", s), sm(7, 16, 32), 4.0, A.mult, [k("sm7c")], [k("sl")], 16, s)
-            zk = [k("zt%d" % z) for z in range(ZS)]
-            for z in range(ZS):
-                a, b = 4 * C * z // ZS, 4 * C * (z + 1) // ZS
-                tt(reg("zt", s, a, b), reg("xh", s).indirect(reg("fl", s, a // 16, b // 16)), reg("xg", s, a, b), A.add, [k("xh"), k("xg"), k("fl")], [zk[z]], b - a, s, gather=True)
+                ts(r("fot"), r("fr"), float(s * C - RO), A.add)
+                dma("Y", T.fo[:, s * C:s * C + C], T.fot[0:128:16, s * C:s * C + C], [r("fot")], [], "stored")
+            scan(r("s4"), reg("amp4"), path, 0.0, A.mult, A.max)
+            for e in range(2):
+                ts(sm(5, e, 2), r("s4", 3 + 4 * e, C, 32), col(17), A.mult, col(13), A.add)
+            tt(sm(6), sm(5), il(2), A.min)
+            sl = r("sl", 0, LW)
+            cp(sl, sm(6))
+            tt(r("zt"), ind(r("xh"), r("fl")), r("xg"), A.add)
+            lin(r("z32"), r("zt"), 32.0)
+            quant(qz, sz, r("zt"))
             for t in range(4):
-                mul(reg("z32", s, t * C, t * C + C), reg("zt", s, t, 4 * C, 4), 32.0, zk, [k("z32%d" % t)], C, s)
-            quant(qz, sz, reg("zt", s), zk, [k("qz")], C, s)
-            for t in range(4):
-                o, bk = bank(s, t)
-                mm(T.ps[:, o:o + C], T.qw[:, 128 * t:128 * t + 128], T.sw[:, 128 * t:128 * t + 128], qz, sz, ["qw", "sw", k("qz")], [bk], C, s)
-                tt(reg("y32", s, t * CW, t * CW + C), T.ps[:, o:o + C], reg("z32", s, t * C, t * C + C), A.add, [k("z32%d" % t)], [bk, k("y%d" % t)], C, s, psum=True)
-                gat(reg("pt", s, t, 4 * SL, 4), reg("y32", s, t * CW, t * CW + C + 1), reg("gl", s, 0, H), [k("y%d" % t), k("gl"), "yz"], [k("pt%d" % t)], SL, s, scale=0.03125)
+                o = bank(s, t, 0, C)
+                mm(o, ("qw", 128 * t, 128 * t + 128, 1), ("sw", 128 * t, 128 * t + 128, 1), qz, sz)
+                tt(r("y32", t, 4 * C, 4), o, r("z32", t, 4 * C, 4), A.add)
+            lin(r("pt", 0, 4 * SL), ind(r("y32"), sl), 0.03125)
             qp, sp = "qp%d" % rd, "sp%d" % rd
-            pts = [k("pt%d" % t) for t in range(4)]
-            quant(reg(qp, s, 0, 128), reg(sp, s, 0, 128), reg("pt", s), pts + ["ptz%d" % s], [k(qp)], 128, s)
+            quant(r(qp, 0, 128), r(sp, 0, 128), r("pt"))
             peer = T.cores[rank ^ STEP[rd]]
             rid, pid, _ = topo.addr(peer)
             mask = topo.mask(core, peer)
@@ -369,54 +348,57 @@ def build(g, T, topo, core, rank):
             ne = len(topo.engines(core, peer))
 
             def send(qp=qp, sp=sp, rid=rid, pid=pid, mask=mask, sem=sem):
-                g.remote_dma(reg(qp, s, 128, QW).bitcast(dt.uint8), reg(qp, s, 0, SL).bitcast(dt.uint8), sem, T.sem.sent, pid, rid, mask)
-                g.remote_dma(reg(sp, s, 128, QW), reg(sp, s, 0, SL), sem, T.sem.sent, pid, rid, mask)
+                g.remote_dma(ap(r(qp, 128, QW)).bitcast(dt.uint8), ap(r(qp, 0, SL)).bitcast(dt.uint8), sem, T.sem.sent, pid, rid, mask)
+                g.remote_dma(ap(r(sp, 128, QW)), ap(r(sp, 0, SL)), sem, T.sem.sent, pid, rid, mask)
                 return None
-            add({"G": (1200.0, send)}, [k(qp)], [k("fly%d" % rd)], s, lat=2200.0, sem="remote", inc=2 * ne)
-            mul(reg("ph", s), reg("pt", s, 0, 4 * SL), 0.5, pts, [k("ph")], 4 * SL, s)
+            fly = add({"G": send}, [r(qp, 0, SL), r(sp, 0, SL)], [], sem="remote", inc=2 * ne)
+            lin(r("ph"), r("pt", 0, 4 * SL), 0.5)
+            lin(X, r("y32", 0, 4 * C), 0.03125)
             for t in range(4):
-                mul(reg("xt", s, t, 4 * C, 4), reg("y32", s, t * CW, t * CW + C), 0.03125, [k("y%d" % t)], [X, k("xw%d" % t)] if t == 0 else [k("xw%d" % t)], C, s)
-                if t > 0:
-                    ops[-1]["r"].append(k("xw0"))
-            for t in range(4):
-                o, bk = bank(s, t)
-                mm(T.ps[:, o:o + 128], T.qe[:, 128 * t:128 * t + 128], T.se[:, 128 * t:128 * t + 128], reg(qp, s, SL, QW), reg(sp, s, SL, QW),
-                   ["qe%d" % t, k(qp), k("fly%d" % rd)], [bk], 128, s, arr=(sem, 2 * ne))
-                tt(reg("hf", s, t * SL, t * SL + SL), T.ps[:, o + 128 - SL:o + 128], reg("ph", s, t, 4 * SL, 4), A.add, [k("ph")], [bk, k("hf%d" % t)], SL, s, psum=True)
-            add({"V": (50 + 3.8 * 4 * SL, lambda: g.vector.tensor_copy(reg("xt", s).indirect(reg("sl", s, 0, 2 * B)), reg("hf", s)))},
-                [k("hf%d" % t) for t in range(4)] + [k("sl")] + [k("xw%d" % t) for t in range(4)], [X], s)
-        quant(qx, sx, reg("xt", s, 0, 4 * C), [X], [k("qx")], C, s)
-        o, bk = bank(s, 0)
-        mm(T.ps[:, o:o + C], T.qv[:], T.sv[:], qx, sx, ["qv", k("qx")], [bk], C, s)
-        add({"V": (cv(C), lambda: g.vector.tensor_copy(reg("yo", s), T.ps[:, o:o + C])),
-             "S": (cv(C) + 30, lambda: g.scalar.activation(reg("yo", s), T.ps[:, o:o + C], F.Copy))}, [], [bk, k("yo")], s)
-        dma("Y", T.oc[:, 4 * s * C:4 * s * C + 4 * C], qx.bitcast(dt.uint8), [k("qx")], [], "stored", 2200, s)
+                mm(bank(s, t, 0, 128), ("qe", 128 * t, 128 * t + 128, 1), ("se", 128 * t, 128 * t + 128, 1), r(qp, SL, QW), r(sp, SL, QW),
+                   arr=(sem, 2 * ne, "%d_%d" % (rd, s)), after=fly)
+                tt(r("hf", t, 4 * SL, 4), bank(s, t, 128 - SL, 128), r("ph", t, 4 * SL, 4), A.add)
+            cp(ind(r("xt"), sl), r("hf"))
+        quant(qx, sx, X)
+        o = bank(s, 0, 0, C)
+        mm(o, reg("qv"), reg("sv"), qx, sx)
+        copy(r("yo"), o)
+        dma("Y", T.oc[:, 4 * s * C:4 * s * C + 4 * C], ap(qx).bitcast(dt.uint8), [qx], [], "stored")
         for q in range(4):
-            dma("Y", T.osc[4 * q:4 * q + 4, s * C:s * C + C], T.sx[32 * q:32 * q + 4, s * C:s * C + C], [k("qx")], [], "stored", 2000, s)
-        dma("S", T.y[:, s * C:s * C + C], reg("yo", s), [k("yo")], [], "stored", 2200, s)
+            dma("Y", T.osc[4 * q:4 * q + 4, s * C:s * C + C], T.sx[32 * q:32 * q + 4, s * C:s * C + C], [sx], [], "stored")
+        dma("S", T.y[:, s * C:s * C + C], ap(r("yo")), [r("yo")], [], "stored")
 
     for s in range(NS):
         stream(s)
     return ops
 
 
+def bits(v, wide):
+    name, a, b, st = v
+    if name == "ps":
+        return 1 << (a // 512)
+    if wide:
+        k = 16 // SIZE[BUF[name][1]]
+        a, b, st = a // k * k, -(-b // k) * k, 1
+    if st in (1, -1):
+        return ((1 << (b - a)) - 1) << a
+    return sum(1 << c for c in range(a, b, st))
+
+
 def deps(ops):
-    last, readers = {}, {}
+    seen = {}
     pred = [set() for _ in ops]
     for i, o in enumerate(ops):
-        for key in o["r"]:
-            if key in last:
-                pred[i].add(last[key])
-        for key in o["w"]:
-            if key in last:
-                pred[i].add(last[key])
-            for j in readers.get(key, []):
-                pred[i].add(j)
-        for key in o["r"]:
-            readers.setdefault(key, []).append(i)
-        for key in o["w"]:
-            last[key] = i
-            readers[key] = []
+        mine = [(v[0], bits(v, o["dma"]), False) for v in o["r"]] + [(v[0], bits(v, o["dma"]), True) for v in o["w"]]
+        for name, m, wr in mine:
+            for j, m2, wr2 in seen.get(name, []):
+                if (wr or wr2) and m & m2:
+                    pred[i].add(j)
+        for name, m, wr in mine:
+            old = seen.get(name, [])
+            if wr:
+                old = [(j, m2 & ~m, wr2) for j, m2, wr2 in old if m2 & ~m]
+            seen[name] = old + [(i, m, wr)]
         pred[i].discard(i)
     return pred
 
@@ -456,12 +438,11 @@ def rank_program(g, core, T, topo):
                     if kn.get(a, 0) < b:
                         kn[a] = b
         if o["arr"] is not None:
-            sem, c = o["arr"]
-            tag = "arr:%s:%s" % (o["r"][-1], e)
-            if tag not in kn:
+            sem, c, tag = o["arr"]
+            if "arr" + tag not in kn:
                 q.wait_ge(sem, c)
-                kn[tag] = 1
-        ins = o["alts"][e][1]()
+                kn["arr" + tag] = 1
+        ins = o["alts"][e]()
         if o["sem"] == "remote":
             count["sent"] = count.get("sent", 0) + o["inc"]
             continue

from concourse.mybir import dt, AluOpType, AxisListType, ActivationFunctionType

A = AluOpType
F = ActivationFunctionType

STEP = [1, 2, 3]
NS = 2
B = 12 // NS
C = 32 * B
CW = C + 16
SL = 8 * B
XW = 4 * C + 4 * SL
QW = 128 + SL
LW = 2 * B
W2W = CW + C
NB = 8 // NS
RO = 16
SH = 144
BIG = 1.0e29
TSINK = 100000.0

ORDER = "070j0o27010800030k09280q0p0r1q0n1h0l0b0m0s261j0w1k0y060x0t160z028729882b190u89250a101a1r0c2a2c0e0f1x201f8a2d3q1i1n2e2f8b9p8c049o3r8d2g8e2h1g0g158f2i8g171z181y1c1d2j110v2k9r2o050i8h1e2l1l3t138i9s2m2p8j1m8m3u2n123v8n0d2q3w8k0h9t2t2r8l142u2s1o2z2w8o303x8p2v8r318q2x1s8s9u1p9q321b2y8x8u8t8y338z8v34908w3591363738923b399v3a933c9495213d963e3g97993h3f1t9a983i239b3l3j9c3m229e3s3k9d1u9f9j3n9g3o3p9h9k3y9i403z9l44411v429m9n45434a461w47489w494b9y4f9xa2a04ha1a34c4o9za84ka44g4d4e4p4la54ia64j4m24a74nad4q4rafae4s4taaaga9abaiacahakajam51al4xanaoap4vaq52ar4w4y4u4zaz50av53axawatb0ayasau5457b158b25559b35ab5b65bb75cb85eb95i5dba5f5g5j56bbbcbd5o5hbgbe5kbhbfbmbi5q5p5lbnbobj5r5m5s5nbk5tbl5ubp5v62605wb4br5ybs63btbubw615x5zc064bvbybxc165bz666b6f67bqc2c3c4c56d6c6e6g6869cbc76a6hcdccc8c9cecac66i6j6lcf6k6mcgcj6nchck6o6pclcmci6q6rcn6s6t6uco6w6vcq74cp6xcucscr6ycvct76d26zcw75d3d4cx7770727178cy79d5cz7b7c7ed77a7f7id97d7j7gd8dc7hdgdd7kdhdadedb7ldfd6didj737m7ndk7o7v7p7r7q7tdl7sdt7wdm7u7xdrdudsdpdqdndo7y817zdvdwe383dx80e2d08285dz86e1dye484d1e0"
ON_V = "1o2b2l2q405e6r7n7o8d9paoarb3bcc2c5chcq"

f32, bf, i32, u16, u8, x4 = "float32", "bfloat16", "int32", "uint16", "uint8", "float8_e4m3fn_x4"
BUF = {
    "fni": (24, i32, 0), "pi": (16, i32, 0), "col": (32, f32, 0), "tmp": (64, f32, 0),
    "iotaR": (CW, bf, 0), "iotaT": (CW, f32, 0), "tw0": (CW, f32, 0), "r16": (C, bf, 0), "r4": (C, bf, 0), "loc": (C, bf, 0), "base": (C, bf, 0),
    "amp": (C, bf, 0), "amp4": (C, bf, 0), "rst": (C, bf, 0), "rmin": (C, bf, 0), "cc": (C, bf, 0),
    "d0": (192, bf, 0), "d1": (192, bf, 0), "d2": (192, bf, 0), "d3": (192, bf, 0), "d4": (192, bf, 0),
    "tbl": (C, bf, 0), "ws0": (CW, bf, 0), "ws1": (CW, bf, 0), "kw": (32, bf, 0), "fix": (16, bf, 0),
    "il": (6 * 16, f32, 0), "li": (16, i32, 0), "cl": (32, u16, 0),
    "zero": (512, bf, 0), "et": (2048, bf, 0), "ut": (512, bf, 0), "vt": (512, bf, 0),
    "qe": (512, x4, 0), "se": (512, u8, 0), "qw": (512, x4, 0), "sw": (512, u8, 0),
    "qu0": (128, x4, 0), "su0": (128, u8, 0), "qu": (128, x4, 0), "su": (128, u8, 0), "qv": (128, x4, 0), "sv": (128, u8, 0),
    "qx": (C, x4, 1), "sx": (C, u8, 1), "qz": (C, x4, 1), "sz": (C, u8, 1),
    "qp0": (QW, x4, 1), "sp0": (QW, u8, 1), "qp1": (QW, x4, 1), "sp1": (QW, u8, 1), "qp2": (QW, x4, 1), "sp2": (QW, u8, 1),
    "xt": (XW, bf, 1), "xh": (4 * C, bf, 1), "xg": (4 * C, bf, 1), "zt": (4 * C, bf, 1), "z32": (4 * C, bf, 1),
    "y32": (XW, bf, 1), "pt": (512, bf, 1), "ph": (4 * SL, bf, 1), "hf": (4 * SL, bf, 1),
    "al": (10 * 16, u16, 1), "ar": (8 * CW, bf, 1), "sb": (C, bf, 1), "s4": (C, bf, 1), "wa": (3 * C, bf, 1), "sc": (2 * C, bf, 1),
    "sm": (8 * 16, f32, 1), "cf": (16, u16, 1), "pos": (16, u16, 1), "kv": (2 * C, bf, 1), "nx": (C, bf, 1),
    "tt": (5 * CW, f32, 1), "tw": (CW, f32, 1),
    "mx": (C, f32, 1), "junk": (C, bf, 1), "hc": (8, f32, 1), "hl": (2, u16, 1),
    "pl": (16, u16, 1), "o2": (16, u16, 1), "fl": (C // 4, u16, 1), "sl": (16, u16, 1),
    "w2": (W2W, bf, 1), "wg": (2 * C, bf, 1), "fr": (C, bf, 1), "fot": (C, f32, 1), "yo": (C, f32, 1),
}
SCRATCH = {k: ("sbuf", [128, v[0] * (NS if v[2] else 1)], v[1]) for k, v in BUF.items()}
SCRATCH["ps"] = ("psum", [128, 4096], f32)
SIZE = {f32: 4, bf: 2, i32: 4, u16: 2, u8: 1, x4: 4}
LOADS = ["fn", "u", "v", "wc", "ws"] + ["x%d" % s for s in range(NS)]
SEMAPHORES = ["cV", "cS", "cP", "cG", "sent", "stored"] + ["ld_" + k for k in LOADS] + ["dup%d" % s for s in range(NS)] + \
    ["arr%d_%d" % (r, s) for r in range(3) for s in range(NS)]


def build(g, T, topo, core, rank):
    ops = []

    def reg(name, s=0, a=0, b=None, step=1):
        w, _, per = BUF[name]
        o = s * w if per else 0
        return (name, o + a, o + (w if b is None else b), step)

    def ap(v):
        if not isinstance(v, tuple):
            return v
        if v[0] == "ind":
            return ap(v[1]).indirect(ap(v[2]))
        name, a, b, st = v
        if st == 1:
            return T[name][:, a:b]
        if st < 0:
            return T[name][:, slice(b - 1, a - 1 if a else None, -1)]
        return T[name][:, a:b:st]

    def ind(win, off):
        return ("ind", win, off)

    def flat(vs):
        out = []
        for v in vs:
            if isinstance(v, tuple):
                out += [v[1], v[2]] if v[0] == "ind" else [v]
        return out

    def add(alts, r, w, sem=None, inc=1, arr=None, after=None, dma=False):
        r, w = flat(r), flat(w)
        w = w + [v for v in r if v[0] == "ps"]
        ops.append({"alts": alts, "r": r, "w": w, "sem": sem, "inc": inc, "arr": arr, "after": after, "dma": dma})
        return len(ops) - 1

    def ts(out, in0, s1, op0, s2=None, op1=None):
        if op1 is None:
            add({"V": lambda: g.vector.tensor_scalar(ap(out), ap(in0), ap(s1), None, op0)}, [in0, s1], [out])
        else:
            add({"V": lambda: g.vector.tensor_scalar(ap(out), ap(in0), ap(s1), ap(s2), op0, op1)}, [in0, s1, s2], [out])

    def tt(out, in0, in1, op):
        add({"V": lambda: g.vector.tensor_tensor(ap(out), ap(in0), ap(in1), op)}, [in0, in1], [out])

    def cp(out, in_):
        add({"V": lambda: g.vector.tensor_copy(ap(out), ap(in_))}, [in_], [out])

    def ms(out, v):
        add({"V": lambda: g.vector.memset(ap(out), v)}, [], [out])

    def red(out, in_, op):
        add({"V": lambda: g.vector.tensor_reduce(ap(out), ap(in_), AxisListType.X, op)}, [in_], [out])

    def scan(out, d0, d1, init, op0, op1):
        add({"V": lambda: g.vector.tensor_tensor_scan(ap(out), ap(d0), ap(d1), init, op0, op1)}, [d0, d1], [out])

    def copy(out, in_):
        add({"V": lambda: g.vector.tensor_copy(ap(out), ap(in_)), "S": lambda: g.scalar.activation(ap(out), ap(in_), F.Copy)}, [in_], [out])

    def gat(out, win, off):
        copy(out, ind(win, off))

    def lin(out, in_, k, c=None):
        if c is None:
            add({"V": lambda: g.vector.tensor_scalar(ap(out), ap(in_), ap(k), None, A.mult),
                 "S": lambda: g.scalar.activation(ap(out), ap(in_), F.Identity, scale=ap(k))}, [in_, k], [out])
        else:
            add({"V": lambda: g.vector.tensor_scalar(ap(out), ap(in_), ap(k), ap(c), A.mult, A.add),
                 "S": lambda: g.scalar.activation(ap(out), ap(in_), F.Identity, scale=ap(k), bias=ap(c))}, [in_, k, c], [out])

    def quant(q, sc, in_):
        add({"V": lambda: g.vector.quantize_mx(ap(q), ap(sc), ap(in_))}, [in_], [q, sc])

    def mm(out, lq, ls, rq, rs, arr=None, after=None):
        add({"P": lambda: g.tensor.matmul_mx(ap(out), ap(lq), ap(ls), ap(rq), ap(rs), True, True)}, [lq, ls, rq, rs], [out], arr=arr, after=after)

    def iota(out, pat, base, cm=0):
        if BUF[out[0]][1] == i32:
            add({"G": lambda: g.iota(ap(out), pat, base, cm)}, [], [out])
        else:
            add({"G": lambda: g.iota(ap(out), pat, base, cm, allow_small_or_imprecise_dtypes=True)}, [], [out])

    def sel(out, in_, pat, op, fill, base, cm):
        add({"G": lambda: g.affine_select(ap(out), ap(in_), pat, op, fill, base, cm)}, [in_], [out])

    def dma(q, out, in_, r, w, sem):
        e = g.sync if q == "Y" else g.scalar
        add({q: lambda: e.dma_start(out, in_)}, r, w, sem=sem, inc=16, dma=True)

    def col(k, n=1):
        return ("col", k, k + n, 1)

    def pi(k, n=1):
        return ("pi", k, k + n, 1)

    def il(m, a=0, step=1):
        return ("il", 16 * m + a, 16 * m + LW, step)

    def bank(s, t, a, b):
        k = s * NB + t % NB
        return ("ps", k * 512 + a, k * 512 + b, 1)

    dma("Y", T.fni[:], T.fn[:], [], [reg("fni")], "ld_fn")
    for s in range(NS):
        v = reg("xt", s, 0, 4 * C)
        dma("S" if s % 2 == 0 else "Y", ap(v), T.x[:, 4 * C * s:4 * C * (s + 1)], [], [v], "ld_x%d" % s)
    dma("S", T.ut[:], T.u[:], [], [reg("ut")], "ld_u")
    dma("Y", T.qw[:].bitcast(dt.uint8), T.wc[:], [], [reg("qw")], "ld_wc")
    dma("Y", T.sw[:], T.ws[:], [], [reg("sw")], "ld_ws")
    dma("Y", T.vt[:], T.v[:], [], [reg("vt")], "ld_v")

    iota(pi(0), [[0, 1]], 0, 1)
    iota(reg("iotaR", 0, 0, C), [[1, C]], RO)
    iota(reg("r16"), [[0, C // 16], [1, 16]], 0)
    iota(reg("loc"), [[0, B], [1, 32]], 0)
    iota(("li", 0, LW, 1), [[0, B], [16, 2]], 0, 1)
    iota(il(0), [[16, LW]], 0)
    iota(reg("iotaT", 0, 0, C), [[1, C]], 0)
    iota(reg("base"), [[32, B], [0, 32]], 0)
    iota(reg("r4"), [[0, C // 4], [1, 4]], 0)
    iota(("kw", 0, 2, 1), [[-1, 2]], 1)
    iota(("kw", 16, 18, 1), [[1, 2]], 0)
    iota(("fix", 0, LW, 1), [[C + RO, 2], [0, B]], 0)
    ts(pi(1), pi(0), 15, A.bitwise_and)
    ts(pi(2), pi(0), 2, A.logical_shift_right, 3, A.bitwise_and)
    ts(pi(3), pi(0), 3, A.bitwise_and)
    ts(pi(4), pi(0), 1, A.logical_shift_right, 7, A.bitwise_and)
    for m in range(4):
        ts(pi(5 + m), pi(0), m, A.logical_shift_right, 1, A.bitwise_and)
    cp(col(0), pi(1))
    cp(col(1, 7), pi(2, 7))
    ts(col(8, 4), col(4, 4), 1024.0, A.mult)
    red(col(12), col(8, 4), A.add)
    ts(col(13), col(2), -4.0 * RO, A.add)
    ts(col(14), col(3), float(B - 1), A.min, 32.0, A.mult)
    ts(col(15), col(4), float(CW), A.mult, col(14), A.add)
    ts(reg("amp"), reg("r16"), col(0), A.is_gt, 16.0, A.mult)
    ts(("tmp", 0, 16, 1), reg("r16", 0, 0, 16), col(0), A.is_le, 0.0625, A.max)
    red(col(16), ("tmp", 0, 16, 1), A.mult)
    ts(reg("amp4"), reg("r4"), col(1), A.is_gt, 16.0, A.mult)
    ts(("tmp", 16, 20, 1), reg("r4", 0, 0, 4), col(1), A.is_le, 0.0625, A.max)
    iota(("tmp", 20, 21, 1), [[0, 1]], 4)
    red(col(17), ("tmp", 16, 21, 1), A.mult)
    ts(reg("rst"), reg("loc"), 0.0, A.not_equal)
    ms(reg("rmin"), 1000.0)
    ts(reg("rmin", 0, 31, C, 32), reg("base", 0, 0, C, 32), float(-SH), A.add)
    ts(reg("cc"), reg("base"), col(14), A.not_equal, -BIG, A.mult)
    ms(reg("iotaR", 0, C, CW), 256.0)
    ms(reg("iotaT", 0, C, CW), TSINK)
    lin(reg("tw0", 0, 0, C + 1), reg("iotaT", 0, 0, C + 1), col(4), col(8))
    ts(il(1), il(0), col(0), A.add, float(-SH), A.add)
    ts(il(2), il(0), col(0), A.add, float(4 * C), A.add)
    ts(il(3), il(0), col(0), A.add, float(CW), A.add)
    cp(("cl", 0, LW, 1), ("li", 0, LW, 1))
    cp(("cl", 16, 24, 1), ("il", 0, 8, 1))
    iota(reg("zero"), [[0, 512]], 0)
    iota(reg("d0", 0, 0, 160), [[0, 160]], 1)
    sel(reg("d1", 0, 0, 144), reg("zero", 0, 0, 144), [[1, 144]], A.not_equal, 1.0, 0, -1)
    sel(reg("d2", 0, 0, 144), reg("d1", 0, 0, 144), [[1, 144]], A.not_equal, -1.0, -16, -1)
    sel(reg("d3", 0, 0, 160), reg("d0", 0, 0, 160), [[-1, 160]], A.is_gt, 0.0, 16, 1)
    sel(reg("d4", 0, 0, 160), reg("d3", 0, 0, 160), [[1, 160]], A.not_equal, float(CW), -16, -1)
    lc = ("cl", 0, LW, 1)
    gat(reg("tbl"), reg("d2", 0, 0, 144), lc)
    gat(reg("ws0", 0, 0, C), reg("d4", 0, 16, 160), lc)
    gat(reg("ws1", 0, 0, C), reg("d4", 0, 0, 144), lc)
    ms(reg("ws0", 0, C, CW), 0.0)
    ms(reg("ws1", 0, C, CW), 0.0)
    for b in range(4):
        sel(("et", 512 * b, 512 * b + 512, 1), reg("zero"), [[8, 128], [1, 4]], A.not_equal, 0.5, -b, -8)
    quant(reg("qe"), reg("se"), reg("et"))
    quant(reg("qu0"), reg("su0"), reg("ut"))
    lu = ("cl", 16, 24, 1)
    add({"V": lambda: g.vector.tensor_copy(T.qu[:].bitcast(dt.uint32), T.qu0[:].bitcast(dt.uint32).indirect(ap(lu)))}, [reg("qu0"), lu], [reg("qu")])
    add({"S": lambda: g.scalar.activation(T.su[:], T.su0[:].indirect(ap(lu)), F.Copy)}, [reg("su0"), lu], [reg("su")])
    quant(reg("qv"), reg("sv"), reg("vt"))
    for s in range(NS):
        iota(reg("pt", s, 4 * SL, 512), [[0, 512 - 4 * SL]], 0)
        iota(reg("y32", s, 4 * C, XW), [[0, 4 * SL]], 0)
    ms(("ar", C, 8 * CW * NS, CW), float(C + RO))
    ms(("w2", C, W2W * NS, W2W), float(C + RO))
    ms(("nx", C - 1, C * NS, C), float(C + RO))
    ms(("tt", C, 5 * CW * NS, CW), TSINK)

    def stream(s):
        def r(name, a=0, b=None, step=1):
            return reg(name, s, a, b, step)

        def al(m):
            return r("al", m * 16, m * 16 + LW)

        def ar(m, n=C):
            return r("ar", m * CW, m * CW + n)

        def tb(m, n=C):
            return r("tt", m * CW, m * CW + n)

        def sm(m, a=0, step=1):
            return r("sm", 16 * m + a, 16 * m + LW, step)

        def tolist(out, row):
            scan(r("sb"), reg("amp"), row, 0.0, A.mult, A.max)
            ts(out, r("sb", 15, C, 16), col(16), A.mult, float(-RO), A.add)

        fs = ("fni", LW * s, LW * (s + 1), 1)
        par = r("w2", 0, C)
        ts(al(0), fs, float(s * C), A.subtract)
        ts(sm(0), fs, float(s * C), A.subtract)
        gat(par, reg("iotaR", 0, 0, C), al(0))
        row = par
        for m in range(4):
            gat(ar(m), row, al(m))
            tolist(al(m + 1), ar(m))
            row = ar(m)
        gat(r("wa", 0, C), reg("tbl"), al(3))
        gat(r("wa", C, 2 * C), r("wa", 0, C), al(3))
        gat(r("wa", 2 * C, 3 * C), r("wa", C, 2 * C), al(4))
        cf = r("cf", 0, LW)
        for e in range(2):
            scan(r("sc", e * C, e * C + C), reg("rst"), r("wa", 2 * C, 3 * C), 0.0, A.mult, A.min if e else A.max)
            ts(r("cf", e, LW, 2), r("sc", e * C + 31, e * C + C, 32), -1.0 if e else 1.0, A.mult)
        gat(r("kv", 0, C), ("kw", 0, 2, 1), cf)
        tt(r("kv", C, 2 * C), ind(("kw", 16, 18, 1), cf), par, A.mult)
        cp(r("kv", 0, 2 * C, 32), ("fix", 0, LW, 1))
        scan(r("nx", 0, C - 1, -1), r("kv", 1, C, -1), r("kv", C + 1, 2 * C, -1), float(C + RO), A.mult, A.add)
        ts(sm(1), cf, 0.0, A.is_equal, 1000.0, A.mult)
        tt(sm(2), sm(1), sm(0), A.add)
        tt(sm(3), sm(2), il(3), A.min)
        cp(r("pos", 0, LW), sm(3))
        cp(ind(r("w2"), r("pos", 0, LW)), r("nx"))
        tolist(al(5), par)
        row = r("w2", 0, C + 1)
        for m in range(4):
            gat(ar(4 + m), row, al(5 + m))
            if m == 0:
                tt(tb(0), ind(reg("tw0", 0, 0, C + 1), al(5)), reg("iotaT", 0, 0, C), A.max)
            else:
                lin(r("tw", 0, C + 1), tb(m - 1, C + 1), col(4 + m), col(8 + m))
                tt(tb(m), ind(r("tw", 0, C + 1), al(5 + m)), tb(m - 1), A.max)
            tolist(al(6 + m), ar(4 + m))
            row = ar(4 + m, C + 1)
        gat(tb(4), tb(3, C + 1), al(9))

        qx, sx, qz, sz = r("qx"), r("sx"), r("qz"), r("sz")
        X = r("xt", 0, 4 * C)
        for rd in range(3):
            quant(qx, sx, X)
            lin(r("xh"), X, 0.5)
            dma("Y", ap(r("xg")), ap(r("xh")), [r("xh")], [r("xg")], "dup%d" % s)
            o = bank(s, 0, 0, C)
            mm(o, reg("qu"), reg("su"), qx, sx)
            scan(r("mx"), o, reg("cc"), -BIG, A.max, A.add)
            red(r("hc", 0, 1), r("mx", 31, C, 32), A.max)
            add({"S": lambda: g.scalar.activation(ap(r("junk")), ap(r("mx")), F.Sign, bias=ap(r("hc", 0, 1)), scale=-1.0, accum_out=ap(r("hc", 4, 5)))},
                [r("mx"), r("hc", 0, 1)], [r("junk"), r("hc", 4, 5)])
            hl = r("hl", 0, 1)
            ts(hl, r("hc", 4, 5), col(15), A.add, float(32 - C), A.add)
            ts(r("pl"), ind(r("tt", 3 * CW, 5 * CW - 16), hl), col(12), A.subtract, float(C), A.min)
            pl = r("pl", 0, LW)
            path = r("w2", CW, W2W)
            for e in range(2):
                gat(r("wg", e * C, e * C + C), reg("ws%d" % e, 0, 0, C + 1), pl)
            gat(path, reg("iotaR", 0, 0, C + 1), pl)
            for e in range(2):
                scan(r("sc", e * C, e * C + C, -1), reg("rmin", 0, 0, C, -1), r("wg", e * C, e * C + C, -1), 1000.0, A.min, A.add)
                tt(sm(4, e, 2), r("sc", e * C, e * C + C, 32), il(1, e, 2), A.max)
            ts(r("o2", 0, LW), sm(4), float(SH), A.add)
            gat(r("fr"), r("w2"), r("o2", 0, LW))
            scan(r("sb"), reg("amp4"), r("fr"), 0.0, A.mult, A.max)
            ts(r("fl"), r("sb", 3, C, 4), col(17), A.mult, col(13), A.add)
            if rd == 2:
                ts(r("fot"), r("fr"), float(s * C - RO), A.add)
                dma("Y", T.fo[:, s * C:s * C + C], T.fot[0:128:16, s * C:s * C + C], [r("fot")], [], "stored")
            scan(r("s4"), reg("amp4"), path, 0.0, A.mult, A.max)
            for e in range(2):
                ts(sm(5, e, 2), r("s4", 3 + 4 * e, C, 32), col(17), A.mult, col(13), A.add)
            tt(sm(6), sm(5), il(2), A.min)
            sl = r("sl", 0, LW)
            cp(sl, sm(6))
            tt(r("zt"), ind(r("xh"), r("fl")), r("xg"), A.add)
            lin(r("z32"), r("zt"), 32.0)
            quant(qz, sz, r("zt"))
            for t in range(4):
                o = bank(s, t, 0, C)
                mm(o, ("qw", 128 * t, 128 * t + 128, 1), ("sw", 128 * t, 128 * t + 128, 1), qz, sz)
                tt(r("y32", t, 4 * C, 4), o, r("z32", t, 4 * C, 4), A.add)
            lin(r("pt", 0, 4 * SL), ind(r("y32"), sl), 0.03125)
            qp, sp = "qp%d" % rd, "sp%d" % rd
            quant(r(qp, 0, 128), r(sp, 0, 128), r("pt"))
            peer = T.cores[rank ^ STEP[rd]]
            rid, pid, _ = topo.addr(peer)
            mask = topo.mask(core, peer)
            sem = T.sem["arr%d_%d" % (rd, s)]
            ne = len(topo.engines(core, peer))

            def send(qp=qp, sp=sp, rid=rid, pid=pid, mask=mask, sem=sem):
                g.remote_dma(ap(r(qp, 128, QW)).bitcast(dt.uint8), ap(r(qp, 0, SL)).bitcast(dt.uint8), sem, T.sem.sent, pid, rid, mask)
                g.remote_dma(ap(r(sp, 128, QW)), ap(r(sp, 0, SL)), sem, T.sem.sent, pid, rid, mask)
                return None
            fly = add({"G": send}, [r(qp, 0, SL), r(sp, 0, SL)], [], sem="remote", inc=2 * ne)
            lin(r("ph"), r("pt", 0, 4 * SL), 0.5)
            lin(X, r("y32", 0, 4 * C), 0.03125)
            for t in range(4):
                mm(bank(s, t, 0, 128), ("qe", 128 * t, 128 * t + 128, 1), ("se", 128 * t, 128 * t + 128, 1), r(qp, SL, QW), r(sp, SL, QW),
                   arr=(sem, 2 * ne, "%d_%d" % (rd, s)), after=fly)
                tt(r("hf", t, 4 * SL, 4), bank(s, t, 128 - SL, 128), r("ph", t, 4 * SL, 4), A.add)
            cp(ind(r("xt"), sl), r("hf"))
        quant(qx, sx, X)
        o = bank(s, 0, 0, C)
        mm(o, reg("qv"), reg("sv"), qx, sx)
        copy(r("yo"), o)
        dma("Y", T.oc[:, 4 * s * C:4 * s * C + 4 * C], ap(qx).bitcast(dt.uint8), [qx], [], "stored")
        for q in range(4):
            dma("Y", T.osc[4 * q:4 * q + 4, s * C:s * C + C], T.sx[32 * q:32 * q + 4, s * C:s * C + C], [sx], [], "stored")
        dma("S", T.y[:, s * C:s * C + C], ap(r("yo")), [r("yo")], [], "stored")

    for s in range(NS):
        stream(s)
    return ops


def bits(v, wide):
    name, a, b, st = v
    if name == "ps":
        return 1 << (a // 512)
    if wide:
        k = 16 // SIZE[BUF[name][1]]
        a, b, st = a // k * k, -(-b // k) * k, 1
    if st in (1, -1):
        return ((1 << (b - a)) - 1) << a
    return sum(1 << c for c in range(a, b, st))


def deps(ops):
    seen = {}
    pred = [set() for _ in ops]
    for i, o in enumerate(ops):
        mine = [(v[0], bits(v, o["dma"]), False) for v in o["r"]] + [(v[0], bits(v, o["dma"]), True) for v in o["w"]]
        for name, m, wr in mine:
            for j, m2, wr2 in seen.get(name, []):
                if (wr or wr2) and m & m2:
                    pred[i].add(j)
        for name, m, wr in mine:
            old = seen.get(name, [])
            if wr:
                old = [(j, m2 & ~m, wr2) for j, m2, wr2 in old if m2 & ~m]
            seen[name] = old + [(i, m, wr)]
        pred[i].discard(i)
    return pred


def digits(text):
    return [int(text[a:a + 2], 36) for a in range(0, len(text), 2)]


def rank_program(g, core, T, topo):
    rank = T.rank_of(core)
    if rank is None:
        return
    ops = build(g, T, topo, core, rank)
    pred = deps(ops)
    order = digits(ORDER) if ORDER else list(range(len(ops)))
    on_v = set(digits(ON_V))
    place = {i: a for a, i in enumerate(order)}
    queue = {"V": g.vector, "S": g.scalar, "P": g.tensor, "G": g, "Y": g.sync}
    count = {}
    mark = [None] * len(ops)
    clock = [None] * len(ops)
    known = {e: {} for e in queue}
    for i in order:
        o = ops[i]
        e = list(o["alts"])[0] if len(o["alts"]) == 1 else ("V" if i in on_v else "S")
        q, kn = queue[e], known[e]
        need = {}
        for j in pred[i]:
            if mark[j] is not None:
                sname, c = mark[j]
                if kn.get(sname, 0) < c and need.get(sname, (0, 0))[0] < c:
                    need[sname] = (c, j)
        for sname, (c, j) in sorted(need.items(), key=lambda kv: -place[kv[1][1]]):
            if kn.get(sname, 0) < c:
                q.wait_ge(T.sem[sname], c)
                for a, b in clock[j].items():
                    if kn.get(a, 0) < b:
                        kn[a] = b
        if o["arr"] is not None:
            sem, c, tag = o["arr"]
            if "arr" + tag not in kn:
                q.wait_ge(sem, c)
                kn["arr" + tag] = 1
        ins = o["alts"][e]()
        if o["sem"] == "remote":
            count["sent"] = count.get("sent", 0) + o["inc"]
            continue
        sname = o["sem"] or "c" + e
        count[sname] = count.get(sname, 0) + o["inc"]
        ins.then_inc(T.sem[sname], o["inc"])
        mark[i] = (sname, count[sname])
        clock[i] = dict(kn)
        clock[i][sname] = count[sname]
    for sname in ["cG", "cP", "cS", "cV", "sent", "stored"]:
        g.wait_ge(T.sem[sname], count[sname])
